import numpy as np
import ml_dtypes


def mxq(x, axis, fmt="e4m3"):
    dtype, down = {"e4m3": (ml_dtypes.float8_e4m3fn, 7), "e5m2": (ml_dtypes.float8_e5m2, 14)}[fmt]
    v = np.moveaxis(np.asarray(x, np.float32).astype(ml_dtypes.bfloat16).astype(np.float64), axis, -1)
    blocks = v.reshape(v.shape[:-1] + (-1, 32))
    amax = np.abs(blocks).max(-1, keepdims=True)
    byte = np.maximum(np.where(amax > 0, np.frexp(amax)[1] - 1 + 127, 0) - down, 1)
    scale = np.exp2(byte - 127.0)
    codes = (blocks / scale).astype(np.float32).astype(dtype).astype(np.float64)
    return np.moveaxis((codes * scale).reshape(v.shape), -1, axis)


WIDE = False


def mx_kscale(k):
    if not WIDE:
        return np.ones(k)
    levels = np.array([24, -24, 12, -12, 0])
    if k % 512:
        return np.exp2(np.random.permutation(np.resize(levels, k // 32))).repeat(32)
    a = np.empty((k // 512, 16))
    for p in range(k // 512):
        a[p, :8] = np.random.permutation(np.resize(levels, 8))
        for g in range(8):
            far = levels[np.abs(levels - a[p, g]) >= 10]
            a[p, g + 8] = far[np.random.randint(len(far))]
    return np.exp2(a.ravel()).repeat(32)


def f64(x):
    return np.asarray(x).astype(np.float64)


def striped(idx):
    return np.tile(idx.reshape(-1, 16).T, (8, 1)).astype(np.uint16)


def unstriped(offs):
    return offs[:16].T.reshape(-1).astype(np.int64)


E2M1 = np.array([0.0, 0.5, 1.0, 1.5, 2.0, 3.0, 4.0, 6.0, -0.0, -0.5, -1.0, -1.5, -2.0, -3.0, -4.0, -6.0])


def pack_weight(w, fmt):
    k, n = w.shape
    w = f64(np.asarray(w, np.float32).astype(ml_dtypes.bfloat16)).reshape(k // 32, 32, n)
    amax = np.abs(w).max(1)
    if fmt == "e4m3":
        byte = np.frexp(amax)[1] - 1 + 127 - 7
    else:
        mant, ex = np.frexp(amax / 6.0)
        byte = np.where(mant > 0.5, ex, ex - 1) + 127
    byte = np.clip(np.where(amax > 0, byte, 1), 1, 254)
    scaled = (w * np.exp2(127.0 - byte)[:, None, :]).reshape(k, n).astype(np.float32)
    by_word = np.ascontiguousarray(scaled.reshape(k // 512, 128, 4, n).transpose(0, 1, 3, 2))
    if fmt == "e4m3":
        words = by_word.astype(ml_dtypes.float8_e4m3fn).view(np.uint8)
    else:
        c = by_word.astype(ml_dtypes.float4_e2m1fn).view(np.uint8) & 0xF
        words = (c[..., 0::2] | (c[..., 1::2] << 4)).reshape(k // 512, 128, 2 * n)
    return np.ascontiguousarray(words), np.ascontiguousarray(byte.astype(np.uint8).reshape(k // 512, 16, n))


def unpack_weight(words, scales, fmt):
    g, _, n = scales.shape
    words = np.ascontiguousarray(words).reshape(g, 128, n, -1)
    if fmt == "e4m3":
        vals = words.view(ml_dtypes.float8_e4m3fn).astype(np.float64)
    else:
        nib = np.empty((g, 128, n, 4), np.uint8)
        nib[..., 0::2] = words & 0xF
        nib[..., 1::2] = words >> 4
        vals = E2M1[nib]
    vals = vals * np.repeat(np.exp2(scales.astype(np.float64) - 127.0), 8, axis=1)[..., None]
    return vals.transpose(0, 1, 3, 2).reshape(g * 512, n)


def split(x):
    m, e = np.frexp(f64(x))
    hi = np.ldexp(np.trunc(16.0 * m) / 16.0, e)
    return hi, f64(x) - hi


K, N, T, J = 512, 256, 4096, 2048


def setup_inputs():
    n = np.random.standard_normal
    s = mx_kscale(K)[:, None]
    p_tab = pack_weight(n((K, T)) * s, "e4m3")
    p_tab2 = pack_weight(n((K, T)) * s, "e4m3")
    p_wi = pack_weight(n((K, N)) / np.sqrt(2 * K) / s, "e2m1")
    return {
        "tab_words": p_tab[0],
        "tab_scales": p_tab[1],
        "tab2_words": p_tab2[0],
        "tab2_scales": p_tab2[1],
        "wr": (n((K, N)) / np.sqrt(2 * K) / s).astype(np.float32),
        "wi_words": p_wi[0],
        "wi_scales": p_wi[1],
        "offs": striped(np.random.permutation(T)[:J]),
    }


def reference(tab_words, tab_scales, tab2_words, tab2_scales, wr, wi_words, wi_scales, offs):
    idx = unstriped(offs)
    tab_ = unpack_weight(tab_words, tab_scales, "e4m3")[:, idx]
    tab2_ = unpack_weight(tab2_words, tab2_scales, "e4m3")[:, idx]
    wr_hi, wr_lo = split(wr)
    wr_hi_, wr_lo_ = mxq(wr_hi, 0, "e4m3"), mxq(wr_lo, 0, "e4m3")
    wi_ = unpack_weight(wi_words, wi_scales, "e2m1")
    rr = wr_hi_.T @ tab_ + wr_lo_.T @ tab_
    ii = wi_.T @ tab2_
    zr = rr - ii
    ri = wr_hi_.T @ tab2_ + wr_lo_.T @ tab2_ + wi_.T @ tab_
    zi = ri
    return np.maximum(zr, 0.0), np.maximum(zi, 0.0)

@@ -1,0 +1,185 @@
+from contextlib import ExitStack
+
+import concourse.mybir as mybir
+
+K, N, T, J = 512, 256, 4096, 2048
+FLOPS = 6 * 2 * K * N * J
+
+F32 = mybir.dt.float32
+BF16 = mybir.dt.bfloat16
+I32 = mybir.dt.int32
+U32 = mybir.dt.uint32
+U16 = mybir.dt.uint16
+U8 = mybir.dt.uint8
+FP8X4 = mybir.dt.float8_e4m3fn_x4
+FP4X4 = mybir.dt.float4_e2m1fn_x4
+ALU = mybir.AluOpType
+ACT = mybir.ActivationFunctionType
+
+P = 128
+PACK = 4
+M = 128
+HALVES = N // M
+W = 512
+SLICES = J // W
+HI_MASK = -(1 << 20)
+
+
+def tile_list_cpxtab_hl_crelu_kernel(
+    tc, tab_words, tab_scales, tab2_words, tab2_scales, wr, wi_words, wi_scales, offs, out_0, out_1
+):
+    nc = tc.nc
+    with ExitStack() as ctx:
+        held = ctx.enter_context(tc.tile_pool(name="held", bufs=1))
+        stage = ctx.enter_context(tc.tile_pool(name="stage", bufs=8))
+        psum = ctx.enter_context(tc.psum_pool(name="psum", bufs=2))
+
+        offsets = held.tile([P, J // 16], U16, name="offsets")
+        nc.sync.dma_start(offsets[:], offs)
+        wr_rows = wr.rearrange("(p j) n -> p j n", j=PACK)
+        raw = []
+        for x in range(2):
+            rows = held.tile([P, 2, N], F32, name=f"raw{x}")
+            nc.sync.dma_start(rows[:], wr_rows[:, 2 * x : 2 * x + 2, :])
+            raw.append(rows)
+
+        def load_scale_rows(name, scales, width):
+            plane = held.tile([P, width // 4], I32, name=name, align_bytes=64)
+            nc.vector.memset(plane[:], 0)
+            for r in range(4):
+                nc.sync.dma_start(plane[r:P:32, :], scales[0, r:16:4, :].bitcast(I32))
+            return plane
+
+        def load_words(name, words):
+            win = held.tile([P, T], I32, name=name, align_bytes=64)
+            nc.sync.dma_start(win[:], words[0].rearrange("p t i -> p (t i)").bitcast(I32))
+            return win
+
+        scale_win = [load_scale_rows("scale_win0", tab_scales, T)]
+        word_win = [load_words("word_win0", tab_words)]
+        wi_codes = held.tile([P, N // 2], I32, name="wi_codes", align_bytes=64)
+        nc.sync.dma_start(wi_codes[:], wi_words[0].bitcast(I32))
+        wi_plane = load_scale_rows("wi_plane", wi_scales, N)
+        scale_win.append(load_scale_rows("scale_win1", tab2_scales, T))
+        word_win.append(load_words("word_win1", tab2_words))
+
+        parts = held.tile([P, 2, PACK, N], F32, name="parts")
+        for x in range(2):
+            rows = slice(2 * x, 2 * x + 2)
+            nc.vector.tensor_scalar(
+                out=parts[:, 0, rows].bitcast(I32),
+                in0=raw[x][:].bitcast(I32),
+                scalar1=HI_MASK,
+                scalar2=None,
+                op0=ALU.bitwise_and,
+            )
+            nc.vector.tensor_tensor(out=parts[:, 1, rows], in0=raw[x][:], in1=parts[:, 0, rows], op=ALU.subtract)
+
+        wq = {}
+        for sign in (-1.0, 1.0):
+            tag = "neg" if sign < 0 else "pos"
+            grouped = held.tile([P, 2, N, PACK], BF16, name=f"grouped_{tag}", align_bytes=64)
+            for h in range(2):
+                nc.scalar.activation(
+                    out=grouped[:, h], in_=parts[:, h].rearrange("p j n -> p n j"), func=ACT.Copy, scale=sign
+                )
+            wq[sign] = grouped
+
+        def quantise(sign):
+            grouped = wq[sign]
+            tag = "scale_win0" if sign < 0 else "codes_pos"
+            codes = held.tile([P, 2 * N], U32, name="codes_neg" if sign < 0 else "codes_pos", tag=tag, align_bytes=64)
+            scales = held.tile([P, 2 * N], U8, name="scales_neg" if sign < 0 else "scales_pos", align_bytes=64)
+            wq[sign] = (grouped, codes, scales)
+            nc.vector.quantize_mx(
+                out=codes[:].bitcast(FP8X4), scales=scales[:], in_=grouped[:].rearrange("p h n j -> p (h n j)")
+            )
+
+        def wr_part(sign, part, half):
+            cols = slice(part * N + half * M, part * N + (half + 1) * M)
+            return wq[sign][1][:, cols].bitcast(FP8X4), wq[sign][2][:, cols]
+
+        def wi_part(half):
+            return (
+                wi_codes[:, half * 64 : (half + 1) * 64].bitcast(FP4X4),
+                wi_plane[:, half * 32 : (half + 1) * 32].bitcast(U8),
+            )
+
+        word_slot = {(0, 0): "A", (0, 1): "B", (1, 0): "C", (1, 1): "D", (1, 2): "E", (0, 2): "C", (0, 3): "D", (1, 3): "C"}
+        sc, wd = {}, {}
+
+        def picks(s):
+            return offsets[:, s * (W // 16) : (s + 1) * (W // 16)]
+
+        def gather_scales(x, s):
+            tag = f"sc0_{s}" if x == 0 else f"sc1_{s % 2}"
+            got = held.tile([P, W], U8, name=f"sc{x}_{s}", tag=tag, align_bytes=64)
+            nc.vector.tensor_copy(got[:], scale_win[x][:].bitcast(U8).indirect(picks(s)))
+            sc[x, s] = got
+
+        def gather_words(x, s):
+            got = held.tile([P, W], U32, name=f"wd{x}_{s}", tag="slot" + word_slot[x, s], align_bytes=64)
+            nc.vector.tensor_copy(got[:], word_win[x][:].bitcast(U32).indirect(picks(s)))
+            wd[x, s] = got
+
+        def operand(x, s):
+            return wd[x, s][:].bitcast(FP8X4), sc[x, s][:]
+
+        def mm(acc, lhs, rhs, start, stop):
+            nc.tensor.matmul_mx(
+                out=acc[:], lhsT=lhs[0], lhsT_scale=lhs[1], rhs=rhs[0], rhs_scale=rhs[1], start=start, stop=stop
+            )
+
+        def finish(acc, sign, out, half, s, on_vector):
+            res = stage.tile([M, W], F32, name="res")
+            if on_vector:
+                nc.vector.tensor_scalar(out=res[:], in0=acc[:], scalar1=sign, scalar2=0.0, op0=ALU.mult, op1=ALU.max)
+            else:
+                nc.scalar.activation(out=res[:], in_=acc[:], func=ACT.Relu, scale=sign)
+            nc.sync.dma_start(out[half * M : (half + 1) * M, s * W : (s + 1) * W], res[:])
+
+        re, im = {}, {}
+
+        def open_sums(s):
+            v = operand(0, s)
+            for h in range(HALVES):
+                re[s, h] = psum.tile([M, W], F32, name=f"re{h}")
+                im[s, h] = psum.tile([M, W], F32, name=f"im{h}")
+                mm(re[s, h], wr_part(-1.0, 0, h), v, True, False)
+                mm(re[s, h], wr_part(-1.0, 1, h), v, False, False)
+            for h in range(HALVES):
+                mm(im[s, h], wi_part(h), v, True, False)
+
+        def close_sums(s):
+            v2 = operand(1, s)
+            last = s == SLICES - 1
+            for h in range(HALVES):
+                mm(re[s, h], wi_part(h), v2, False, True)
+                finish(re[s, h], -1.0, out_0, h, s, last and h == 1)
+            for h in range(HALVES):
+                mm(im[s, h], wr_part(1.0, 0, h), v2, False, False)
+                mm(im[s, h], wr_part(1.0, 1, h), v2, False, True)
+                finish(im[s, h], 1.0, out_1, h, s, last and h == 1)
+
+        for s in range(SLICES):
+            gather_scales(0, s)
+        quantise(-1.0)
+        for s in (0, 1):
+            gather_words(0, s)
+            open_sums(s)
+        quantise(1.0)
+        for s in (0, 1):
+            gather_scales(1, s)
+        for s in (0, 1):
+            gather_words(1, s)
+            close_sums(s)
+        gather_words(1, 2)
+        gather_words(0, 2)
+        open_sums(2)
+        gather_scales(1, 2)
+        close_sums(2)
+        gather_words(0, 3)
+        open_sums(3)
+        gather_scales(1, 3)
+        gather_words(1, 3)
+        close_sums(3)

@@ -43,24 +43,30 @@ def tile_list_cpxtab_hl_crelu_kernel(
             nc.sync.dma_start(rows[:], wr_rows[:, 2 * x : 2 * x + 2, :])
             raw.append(rows)
 
-        def load_scale_rows(name, scales, width):
+        def zeroed_plane(name, width):
             plane = held.tile([P, width // 4], I32, name=name, align_bytes=64)
             nc.vector.memset(plane[:], 0)
-            for r in range(4):
-                nc.sync.dma_start(plane[r:P:32, :], scales[0, r:16:4, :].bitcast(I32))
             return plane
+
+        def load_scale_rows(plane, scales, rows):
+            for r in rows:
+                nc.sync.dma_start(plane[r:P:32, :], scales[0, r:16:4, :].bitcast(I32))
 
         def load_words(name, words):
             win = held.tile([P, T], I32, name=name, align_bytes=64)
             nc.sync.dma_start(win[:], words[0].rearrange("p t i -> p (t i)").bitcast(I32))
             return win
 
-        scale_win = [load_scale_rows("scale_win0", tab_scales, T)]
-        word_win = [load_words("word_win0", tab_words)]
+        scale_win = [zeroed_plane("scale_win0", T)]
+        wi_plane = zeroed_plane("wi_plane", N)
+        scale_win.append(zeroed_plane("scale_win1", T))
+        load_scale_rows(scale_win[0], tab_scales, range(4))
         wi_codes = held.tile([P, N // 2], I32, name="wi_codes", align_bytes=64)
         nc.sync.dma_start(wi_codes[:], wi_words[0].bitcast(I32))
-        wi_plane = load_scale_rows("wi_plane", wi_scales, N)
-        scale_win.append(load_scale_rows("scale_win1", tab2_scales, T))
+        load_scale_rows(wi_plane, wi_scales, range(0, 2))
+        word_win = [load_words("word_win0", tab_words)]
+        load_scale_rows(wi_plane, wi_scales, range(2, 4))
+        load_scale_rows(scale_win[1], tab2_scales, range(4))
         word_win.append(load_words("word_win1", tab2_words))
 
         parts = held.tile([P, 2, PACK, N], F32, name="parts")
@@ -112,10 +118,10 @@ def tile_list_cpxtab_hl_crelu_kernel(
             return offsets[:, s * (W // 16) : (s + 1) * (W // 16)]
 
         def gather_scales(x, s):
-            tag = f"sc0_{s}" if x == 0 else f"sc1_{s % 2}"
+            tag = f"sc1_{s % 2}"
             got = held.tile([P, W], U8, name=f"sc{x}_{s}", tag=tag, align_bytes=64)
             nc.vector.tensor_copy(got[:], scale_win[x][:].bitcast(U8).indirect(picks(s)))
-            sc[x, s] = got
+            sc[x, s] = got[:]
 
         def gather_words(x, s):
             got = held.tile([P, W], U32, name=f"wd{x}_{s}", tag="slot" + word_slot[x, s], align_bytes=64)
@@ -123,7 +129,7 @@ def tile_list_cpxtab_hl_crelu_kernel(
             wd[x, s] = got
 
         def operand(x, s):
-            return wd[x, s][:].bitcast(FP8X4), sc[x, s][:]
+            return wd[x, s][:].bitcast(FP8X4), sc[x, s]
 
         def mm(acc, lhs, rhs, start, stop):
             nc.tensor.matmul_mx(
@@ -161,8 +167,10 @@ def tile_list_cpxtab_hl_crelu_kernel(
                 mm(im[s, h], wr_part(1.0, 1, h), v2, False, True)
                 finish(im[s, h], 1.0, out_1, h, s, last and h == 1)
 
+        sc_all = held.tile([P, J], U8, name="sc_all", align_bytes=64)
+        nc.vector.tensor_copy(sc_all[:], scale_win[0][:].bitcast(U8).indirect(offsets[:]))
         for s in range(SLICES):
-            gather_scales(0, s)
+            sc[0, s] = sc_all[:, s * W : (s + 1) * W]
         quantise(-1.0)
         for s in (0, 1):
             gather_words(0, s)

@@ -32,7 +32,7 @@ def tile_list_cpxtab_hl_crelu_kernel(
     with ExitStack() as ctx:
         held = ctx.enter_context(tc.tile_pool(name="held", bufs=1))
         stage = ctx.enter_context(tc.tile_pool(name="stage", bufs=8))
-        psum = ctx.enter_context(tc.psum_pool(name="psum", bufs=2))
+        psum = ctx.enter_context(tc.psum_pool(name="psum", bufs=1))
 
         offsets = held.tile([P, J // 16], U16, name="offsets")
         nc.sync.dma_start(offsets[:], offs)
@@ -61,13 +61,12 @@ def tile_list_cpxtab_hl_crelu_kernel(
         wi_plane = zeroed_plane("wi_plane", N)
         scale_win.append(zeroed_plane("scale_win1", T))
         load_scale_rows(scale_win[0], tab_scales, range(4))
+        word_win = [load_words("word_win0", tab_words)]
         wi_codes = held.tile([P, N // 2], I32, name="wi_codes", align_bytes=64)
         nc.sync.dma_start(wi_codes[:], wi_words[0].bitcast(I32))
-        load_scale_rows(wi_plane, wi_scales, range(0, 2))
-        word_win = [load_words("word_win0", tab_words)]
-        load_scale_rows(wi_plane, wi_scales, range(2, 4))
         load_scale_rows(scale_win[1], tab2_scales, range(4))
         word_win.append(load_words("word_win1", tab2_words))
+        load_scale_rows(wi_plane, wi_scales, range(4))
 
         parts = held.tile([P, 2, PACK, N], F32, name="parts")
         for x in range(2):
@@ -81,29 +80,28 @@ def tile_list_cpxtab_hl_crelu_kernel(
             )
             nc.vector.tensor_tensor(out=parts[:, 1, rows], in0=raw[x][:], in1=parts[:, 0, rows], op=ALU.subtract)
 
-        wq = {}
-        for sign in (-1.0, 1.0):
-            tag = "neg" if sign < 0 else "pos"
-            grouped = held.tile([P, 2, N, PACK], BF16, name=f"grouped_{tag}", align_bytes=64)
+        grouped = held.tile([P, 2, 2, N, PACK], BF16, name="grouped", align_bytes=64)
+        for x, sign in enumerate((-1.0, 1.0)):
             for h in range(2):
                 nc.scalar.activation(
-                    out=grouped[:, h], in_=parts[:, h].rearrange("p j n -> p n j"), func=ACT.Copy, scale=sign
+                    out=grouped[:, x, h], in_=parts[:, h].rearrange("p j n -> p n j"), func=ACT.Copy, scale=sign
                 )
-            wq[sign] = grouped
 
-        def quantise(sign):
-            grouped = wq[sign]
-            tag = "scale_win0" if sign < 0 else "codes_pos"
-            codes = held.tile([P, 2 * N], U32, name="codes_neg" if sign < 0 else "codes_pos", tag=tag, align_bytes=64)
-            scales = held.tile([P, 2 * N], U8, name="scales_neg" if sign < 0 else "scales_pos", align_bytes=64)
-            wq[sign] = (grouped, codes, scales)
+        wq = {}
+
+        def quantise():
+            wq["codes"] = held.tile([P, 4 * N], U32, name="codes", tag="scale_win0", align_bytes=64)
+            wq["scales"] = held.tile([P, 4 * N], U8, name="wr_scales", align_bytes=64)
             nc.vector.quantize_mx(
-                out=codes[:].bitcast(FP8X4), scales=scales[:], in_=grouped[:].rearrange("p h n j -> p (h n j)")
+                out=wq["codes"][:].bitcast(FP8X4),
+                scales=wq["scales"][:],
+                in_=grouped[:].rearrange("p x h n j -> p (x h n j)"),
             )
 
         def wr_part(sign, part, half):
-            cols = slice(part * N + half * M, part * N + (half + 1) * M)
-            return wq[sign][1][:, cols].bitcast(FP8X4), wq[sign][2][:, cols]
+            first = (0 if sign < 0 else 2 * N) + part * N + half * M
+            cols = slice(first, first + M)
+            return wq["codes"][:, cols].bitcast(FP8X4), wq["scales"][:, cols]
 
         def wi_part(half):
             return (
@@ -111,20 +109,18 @@ def tile_list_cpxtab_hl_crelu_kernel(
                 wi_plane[:, half * 32 : (half + 1) * 32].bitcast(U8),
             )
 
-        word_slot = {(0, 0): "A", (0, 1): "B", (1, 0): "C", (1, 1): "D", (1, 2): "E", (0, 2): "C", (0, 3): "D", (1, 3): "C"}
         sc, wd = {}, {}
 
         def picks(s):
             return offsets[:, s * (W // 16) : (s + 1) * (W // 16)]
 
-        def gather_scales(x, s):
-            tag = f"sc1_{s % 2}"
-            got = held.tile([P, W], U8, name=f"sc{x}_{s}", tag=tag, align_bytes=64)
+        def gather_scales(x, s, slot):
+            got = held.tile([P, W], U8, name=f"sc{x}_{s}", tag=slot, align_bytes=64)
             nc.vector.tensor_copy(got[:], scale_win[x][:].bitcast(U8).indirect(picks(s)))
             sc[x, s] = got[:]
 
-        def gather_words(x, s):
-            got = held.tile([P, W], U32, name=f"wd{x}_{s}", tag="slot" + word_slot[x, s], align_bytes=64)
+        def gather_words(x, s, slot):
+            got = held.tile([P, W], U32, name=f"wd{x}_{s}", tag=slot, align_bytes=64)
             nc.vector.tensor_copy(got[:], word_win[x][:].bitcast(U32).indirect(picks(s)))
             wd[x, s] = got
 
@@ -146,48 +142,55 @@ def tile_list_cpxtab_hl_crelu_kernel(
 
         re, im = {}, {}
 
-        def open_sums(s):
-            v = operand(0, s)
+        def open_re(s, pair):
             for h in range(HALVES):
-                re[s, h] = psum.tile([M, W], F32, name=f"re{h}")
-                im[s, h] = psum.tile([M, W], F32, name=f"im{h}")
-                mm(re[s, h], wr_part(-1.0, 0, h), v, True, False)
-                mm(re[s, h], wr_part(-1.0, 1, h), v, False, False)
-            for h in range(HALVES):
-                mm(im[s, h], wi_part(h), v, True, False)
+                re[s, h] = psum.tile([M, W], F32, name=f"re{s}_{h}", tag=f"bank{pair}_{h}")
+                mm(re[s, h], wr_part(-1.0, 0, h), operand(0, s), True, False)
+                mm(re[s, h], wr_part(-1.0, 1, h), operand(0, s), False, False)
 
-        def close_sums(s):
-            v2 = operand(1, s)
-            last = s == SLICES - 1
+        def open_im(s, pair):
             for h in range(HALVES):
-                mm(re[s, h], wi_part(h), v2, False, True)
-                finish(re[s, h], -1.0, out_0, h, s, last and h == 1)
+                im[s, h] = psum.tile([M, W], F32, name=f"im{s}_{h}", tag=f"bank{pair}_{h}")
+                mm(im[s, h], wi_part(h), operand(0, s), True, False)
+
+        def close_re(s):
             for h in range(HALVES):
-                mm(im[s, h], wr_part(1.0, 0, h), v2, False, False)
-                mm(im[s, h], wr_part(1.0, 1, h), v2, False, True)
-                finish(im[s, h], 1.0, out_1, h, s, last and h == 1)
+                mm(re[s, h], wi_part(h), operand(1, s), False, True)
+                finish(re[s, h], -1.0, out_0, h, s, s == SLICES - 1 and h == 1)
+
+        def close_im(s):
+            for h in range(HALVES):
+                mm(im[s, h], wr_part(1.0, 0, h), operand(1, s), False, False)
+                mm(im[s, h], wr_part(1.0, 1, h), operand(1, s), False, True)
+                finish(im[s, h], 1.0, out_1, h, s, s == SLICES - 1 and h == 1)
 
         sc_all = held.tile([P, J], U8, name="sc_all", align_bytes=64)
         nc.vector.tensor_copy(sc_all[:], scale_win[0][:].bitcast(U8).indirect(offsets[:]))
         for s in range(SLICES):
             sc[0, s] = sc_all[:, s * W : (s + 1) * W]
-        quantise(-1.0)
-        for s in (0, 1):
-            gather_words(0, s)
-            open_sums(s)
-        quantise(1.0)
-        for s in (0, 1):
-            gather_scales(1, s)
-        for s in (0, 1):
-            gather_words(1, s)
-            close_sums(s)
-        gather_words(1, 2)
-        gather_words(0, 2)
-        open_sums(2)
-        gather_scales(1, 2)
-        close_sums(2)
-        gather_words(0, 3)
-        open_sums(3)
-        gather_scales(1, 3)
-        gather_words(1, 3)
-        close_sums(3)
+        quantise()
+        for s in range(3):
+            gather_words(0, s, f"slot{s}")
+            open_re(s, s)
+        open_im(0, 3)
+        gather_scales(1, 0, "slot3")
+        gather_words(1, 0, "slot4")
+        close_re(0)
+        close_im(0)
+        open_im(1, 0)
+        gather_words(1, 1, "slot5")
+        gather_scales(1, 1, "slot0")
+        close_re(1)
+        close_im(1)
+        open_im(2, 3)
+        gather_words(1, 2, "slot4")
+        gather_scales(1, 2, "slot3")
+        close_re(2)
+        close_im(2)
+        gather_words(0, 3, "slot1")
+        open_re(3, 1)
+        open_im(3, 0)
+        gather_scales(1, 3, "slot0")
+        gather_words(1, 3, "slot5")
+        close_re(3)
+        close_im(3)

@@ -58,15 +58,17 @@ def tile_list_cpxtab_hl_crelu_kernel(
             return win
 
         scale_win = [zeroed_plane("scale_win0", T)]
-        wi_plane = zeroed_plane("wi_plane", N)
+        shared_plane = zeroed_plane("shared_plane", 2 * N)
+        wi_plane = shared_plane[:, : N // 4]
         scale_win.append(zeroed_plane("scale_win1", T))
         load_scale_rows(scale_win[0], tab_scales, range(4))
+        load_scale_rows(wi_plane, wi_scales, range(0, 3))
         word_win = [load_words("word_win0", tab_words)]
-        wi_codes = held.tile([P, N // 2], I32, name="wi_codes", align_bytes=64)
-        nc.sync.dma_start(wi_codes[:], wi_words[0].bitcast(I32))
+        load_scale_rows(wi_plane, wi_scales, range(3, 4))
         load_scale_rows(scale_win[1], tab2_scales, range(4))
         word_win.append(load_words("word_win1", tab2_words))
-        load_scale_rows(wi_plane, wi_scales, range(4))
+        wi_codes = held.tile([P, N // 2], I32, name="wi_codes", align_bytes=64)
+        nc.sync.dma_start(wi_codes[:], wi_words[0].bitcast(I32))
 
         parts = held.tile([P, 2, PACK, N], F32, name="parts")
         for x in range(2):
@@ -80,28 +82,32 @@ def tile_list_cpxtab_hl_crelu_kernel(
             )
             nc.vector.tensor_tensor(out=parts[:, 1, rows], in0=raw[x][:], in1=parts[:, 0, rows], op=ALU.subtract)
 
-        grouped = held.tile([P, 2, 2, N, PACK], BF16, name="grouped", align_bytes=64)
-        for x, sign in enumerate((-1.0, 1.0)):
+        grouped, codes, code_scales = {}, {}, {}
+        for sign in (-1, 1):
+            grouped[sign] = held.tile([P, 2, N, PACK], BF16, name=f"grouped{sign + 1}", align_bytes=64)
             for h in range(2):
                 nc.scalar.activation(
-                    out=grouped[:, x, h], in_=parts[:, h].rearrange("p j n -> p n j"), func=ACT.Copy, scale=sign
+                    out=grouped[sign][:, h],
+                    in_=parts[:, h].rearrange("p j n -> p n j"),
+                    func=ACT.Copy,
+                    scale=float(sign),
                 )
 
-        wq = {}
-
-        def quantise():
-            wq["codes"] = held.tile([P, 4 * N], U32, name="codes", tag="scale_win0", align_bytes=64)
-            wq["scales"] = held.tile([P, 4 * N], U8, name="wr_scales", align_bytes=64)
+        def quantise(sign, slot):
+            codes[sign] = held.tile([P, 2 * N], U32, name=f"codes{sign + 1}", tag=slot, align_bytes=64)
+            if sign < 0:
+                code_scales[sign] = held.tile([P, 2 * N], U8, name="neg_scales", align_bytes=64)[:]
+            else:
+                code_scales[sign] = shared_plane[4:P, :].bitcast(U8)
             nc.vector.quantize_mx(
-                out=wq["codes"][:].bitcast(FP8X4),
-                scales=wq["scales"][:],
-                in_=grouped[:].rearrange("p x h n j -> p (x h n j)"),
+                out=codes[sign][:].bitcast(FP8X4),
+                scales=code_scales[sign],
+                in_=grouped[sign][:].rearrange("p h n j -> p (h n j)"),
             )
 
         def wr_part(sign, part, half):
-            first = (0 if sign < 0 else 2 * N) + part * N + half * M
-            cols = slice(first, first + M)
-            return wq["codes"][:, cols].bitcast(FP8X4), wq["scales"][:, cols]
+            cols = slice(part * N + half * M, part * N + (half + 1) * M)
+            return codes[sign][:, cols].bitcast(FP8X4), code_scales[sign][:, cols]
 
         def wi_part(half):
             return (
@@ -145,8 +151,8 @@ def tile_list_cpxtab_hl_crelu_kernel(
         def open_re(s, pair):
             for h in range(HALVES):
                 re[s, h] = psum.tile([M, W], F32, name=f"re{s}_{h}", tag=f"bank{pair}_{h}")
-                mm(re[s, h], wr_part(-1.0, 0, h), operand(0, s), True, False)
-                mm(re[s, h], wr_part(-1.0, 1, h), operand(0, s), False, False)
+                mm(re[s, h], wr_part(-1, 0, h), operand(0, s), True, False)
+                mm(re[s, h], wr_part(-1, 1, h), operand(0, s), False, False)
 
         def open_im(s, pair):
             for h in range(HALVES):
@@ -160,18 +166,19 @@ def tile_list_cpxtab_hl_crelu_kernel(
 
         def close_im(s):
             for h in range(HALVES):
-                mm(im[s, h], wr_part(1.0, 0, h), operand(1, s), False, False)
-                mm(im[s, h], wr_part(1.0, 1, h), operand(1, s), False, True)
+                mm(im[s, h], wr_part(1, 0, h), operand(1, s), False, False)
+                mm(im[s, h], wr_part(1, 1, h), operand(1, s), False, True)
                 finish(im[s, h], 1.0, out_1, h, s, s == SLICES - 1 and h == 1)
 
         sc_all = held.tile([P, J], U8, name="sc_all", align_bytes=64)
         nc.vector.tensor_copy(sc_all[:], scale_win[0][:].bitcast(U8).indirect(offsets[:]))
         for s in range(SLICES):
             sc[0, s] = sc_all[:, s * W : (s + 1) * W]
-        quantise()
+        quantise(-1, "scale_win0")
         for s in range(3):
             gather_words(0, s, f"slot{s}")
             open_re(s, s)
+        quantise(1, "codes_pos")
         open_im(0, 3)
         gather_scales(1, 0, "slot3")
         gather_words(1, 0, "slot4")

@@ -48,9 +48,9 @@ def tile_list_cpxtab_hl_crelu_kernel(
             nc.vector.memset(plane[:], 0)
             return plane
 
-        def load_scale_rows(plane, scales, rows):
+        def load_scale_rows(plane, scales, rows, down=0):
             for r in rows:
-                nc.sync.dma_start(plane[r:P:32, :], scales[0, r:16:4, :].bitcast(I32))
+                nc.sync.dma_start(plane[down + r : P : 32, :], scales[0, r:16:4, :].bitcast(I32))
 
         def load_words(name, words):
             win = held.tile([P, T], I32, name=name, align_bytes=64)
@@ -59,16 +59,15 @@ def tile_list_cpxtab_hl_crelu_kernel(
 
         scale_win = [zeroed_plane("scale_win0", T)]
         shared_plane = zeroed_plane("shared_plane", 2 * N)
-        wi_plane = shared_plane[:, : N // 4]
         scale_win.append(zeroed_plane("scale_win1", T))
-        load_scale_rows(scale_win[0], tab_scales, range(4))
-        load_scale_rows(wi_plane, wi_scales, range(0, 3))
+        wi_plane = shared_plane[:, : N // 4]
+        low_plane = zeroed_plane("low_plane", J)
+        load_scale_rows(scale_win[0], tab_scales, range(4), 4)
+        load_scale_rows(scale_win[1], tab2_scales, range(0, 3))
         word_win = [load_words("word_win0", tab_words)]
-        load_scale_rows(wi_plane, wi_scales, range(3, 4))
-        load_scale_rows(scale_win[1], tab2_scales, range(4))
+        load_scale_rows(scale_win[1], tab2_scales, range(3, 4))
+        load_scale_rows(wi_plane, wi_scales, range(4))
         word_win.append(load_words("word_win1", tab2_words))
-        wi_codes = held.tile([P, N // 2], I32, name="wi_codes", align_bytes=64)
-        nc.sync.dma_start(wi_codes[:], wi_words[0].bitcast(I32))
 
         parts = held.tile([P, 2, PACK, N], F32, name="parts")
         for x in range(2):
@@ -157,7 +156,8 @@ def tile_list_cpxtab_hl_crelu_kernel(
         def open_im(s, pair):
             for h in range(HALVES):
                 im[s, h] = psum.tile([M, W], F32, name=f"im{s}_{h}", tag=f"bank{pair}_{h}")
-                mm(im[s, h], wi_part(h), operand(0, s), True, False)
+                low = low_plane[:, s * W // 4 : (s + 1) * W // 4].bitcast(U8)
+                mm(im[s, h], wi_part(h), (operand(0, s)[0], low), True, False)
 
         def close_re(s):
             for h in range(HALVES):
@@ -173,31 +173,37 @@ def tile_list_cpxtab_hl_crelu_kernel(
         sc_all = held.tile([P, J], U8, name="sc_all", align_bytes=64)
         nc.vector.tensor_copy(sc_all[:], scale_win[0][:].bitcast(U8).indirect(offsets[:]))
         for s in range(SLICES):
-            sc[0, s] = sc_all[:, s * W : (s + 1) * W]
+            sc[0, s] = sc_all[4:P, s * W : (s + 1) * W]
+        for r in range(4):
+            nc.sync.dma_start(low_plane[r:P:32, :], sc_all[4 + r : P : 32, :].bitcast(I32))
+        wi_codes = held.tile([P, N // 2], I32, name="wi_codes", align_bytes=64)
+        nc.sync.dma_start(wi_codes[:], wi_words[0].bitcast(I32))
         quantise(-1, "scale_win0")
-        for s in range(3):
+        for s in range(2):
             gather_words(0, s, f"slot{s}")
             open_re(s, s)
-        quantise(1, "codes_pos")
-        open_im(0, 3)
         gather_scales(1, 0, "slot3")
+        quantise(1, "codes_pos")
+        open_im(0, 2)
         gather_words(1, 0, "slot4")
         close_re(0)
         close_im(0)
-        open_im(1, 0)
+        open_im(1, 3)
         gather_words(1, 1, "slot5")
         gather_scales(1, 1, "slot0")
         close_re(1)
         close_im(1)
-        open_im(2, 3)
-        gather_words(1, 2, "slot4")
-        gather_scales(1, 2, "slot3")
+        gather_words(0, 2, "slot4")
+        open_re(2, 0)
+        open_im(2, 2)
+        gather_words(1, 2, "slot3")
+        gather_scales(1, 2, "slot1")
         close_re(2)
         close_im(2)
-        gather_words(0, 3, "slot1")
+        gather_words(0, 3, "slot5")
         open_re(3, 1)
-        open_im(3, 0)
+        open_im(3, 3)
         gather_scales(1, 3, "slot0")
-        gather_words(1, 3, "slot5")
+        gather_words(1, 3, "slot4")
         close_re(3)
         close_im(3)

@@ -22,6 +22,8 @@ M = 128
 HALVES = N // M
 W = 512
 SLICES = J // W
+ROWS = 16
+TOP = P - ROWS
 HI_MASK = -(1 << 20)
 
 
@@ -31,55 +33,67 @@ def tile_list_cpxtab_hl_crelu_kernel(
     nc = tc.nc
     with ExitStack() as ctx:
         held = ctx.enter_context(tc.tile_pool(name="held", bufs=1))
+        reused = ctx.enter_context(tc.tile_pool(name="reused", bufs=1))
         stage = ctx.enter_context(tc.tile_pool(name="stage", bufs=8))
         psum = ctx.enter_context(tc.psum_pool(name="psum", bufs=1))
 
         offsets = held.tile([P, J // 16], U16, name="offsets")
         nc.sync.dma_start(offsets[:], offs)
-        wr_rows = wr.rearrange("(p j) n -> p j n", j=PACK)
-        raw = []
-        for x in range(2):
-            rows = held.tile([P, 2, N], F32, name=f"raw{x}")
-            nc.sync.dma_start(rows[:], wr_rows[:, 2 * x : 2 * x + 2, :])
-            raw.append(rows)
 
-        def zeroed_plane(name, width):
-            plane = held.tile([P, width // 4], I32, name=name, align_bytes=64)
+        scale_win = [held.tile([P, T // 4], I32, name=f"scale_win{x}", align_bytes=64) for x in range(2)]
+        nc.vector.memset(scale_win[1][:], 0)
+        nc.vector.memset(scale_win[0][:TOP], 0)
+        nc.sync.dma_start(scale_win[0][TOP:], tab_scales[0].bitcast(I32))
+        raw = reused.tile([P, PACK, N], F32, name="raw", offset=0, align_bytes=64)
+        nc.sync.dma_start(raw[:], wr.rearrange("(p j) n -> p j n", j=PACK))
+        for r in range(4):
+            nc.sync.dma_start(scale_win[1][r:P:32, :], tab2_scales[0, r:16:4, :].bitcast(I32))
+        planes = [held.tile([P, J // 8], I32, name=f"plane{half}", align_bytes=64) for half in range(2)]
+        for plane in planes:
             nc.vector.memset(plane[:], 0)
-            return plane
 
-        def load_scale_rows(plane, scales, rows, down=0):
-            for r in rows:
-                nc.sync.dma_start(plane[down + r : P : 32, :], scales[0, r:16:4, :].bitcast(I32))
+        wi_plane = held.tile([P, N // 4], I32, name="wi_plane", align_bytes=64)
+        nc.gpsimd.memset(wi_plane[:], 0)
+        for r in range(4):
+            nc.gpsimd.dma_start(wi_plane[r:P:32, :], wi_scales[0, r:16:4, :].bitcast(I32))
 
-        def load_words(name, words):
-            win = held.tile([P, T], I32, name=name, align_bytes=64)
+        def load_words(win, words):
             nc.sync.dma_start(win[:], words[0].rearrange("p t i -> p (t i)").bitcast(I32))
-            return win
 
-        scale_win = [zeroed_plane("scale_win0", T)]
-        shared_plane = zeroed_plane("shared_plane", 2 * N)
-        scale_win.append(zeroed_plane("scale_win1", T))
-        wi_plane = shared_plane[:, : N // 4]
-        low_plane = zeroed_plane("low_plane", J)
-        load_scale_rows(scale_win[0], tab_scales, range(4), 4)
-        load_scale_rows(scale_win[1], tab2_scales, range(0, 3))
-        word_win = [load_words("word_win0", tab_words)]
-        load_scale_rows(scale_win[1], tab2_scales, range(3, 4))
-        load_scale_rows(wi_plane, wi_scales, range(4))
-        word_win.append(load_words("word_win1", tab2_words))
+        word_win = [held.tile([P, T], I32, name="word_win0", align_bytes=64)]
+        load_words(word_win[0], tab_words)
+
+        def picks(first, count):
+            return offsets[:, first // 16 : (first + count) // 16]
+
+        def gather_top_rows(got, half):
+            nc.vector.tensor_copy(got[:], scale_win[0][:].bitcast(U8).indirect(picks(half * J // 2, J // 2)))
+
+        def deal_top_rows(got, half):
+            for r in range(4):
+                nc.sync.dma_start(planes[half][r:P:32, :], got[TOP + r : P : 4, :].bitcast(I32))
+
+        top0 = held.tile([P, J // 2], U8, name="top0", tag="top0", align_bytes=64)
+        gather_top_rows(top0, 0)
+        deal_top_rows(top0, 0)
 
         parts = held.tile([P, 2, PACK, N], F32, name="parts")
-        for x in range(2):
-            rows = slice(2 * x, 2 * x + 2)
-            nc.vector.tensor_scalar(
-                out=parts[:, 0, rows].bitcast(I32),
-                in0=raw[x][:].bitcast(I32),
-                scalar1=HI_MASK,
-                scalar2=None,
-                op0=ALU.bitwise_and,
-            )
-            nc.vector.tensor_tensor(out=parts[:, 1, rows], in0=raw[x][:], in1=parts[:, 0, rows], op=ALU.subtract)
+        nc.vector.tensor_scalar(
+            out=parts[:, 0].bitcast(I32),
+            in0=raw[:].bitcast(I32),
+            scalar1=HI_MASK,
+            scalar2=None,
+            op0=ALU.bitwise_and,
+        )
+        nc.vector.tensor_tensor(out=parts[:, 1], in0=raw[:], in1=parts[:, 0], op=ALU.subtract)
+
+        word_win.append(held.tile([P, T], I32, name="word_win1", align_bytes=64))
+        load_words(word_win[1], tab2_words)
+        top1 = reused.tile([P, J // 2], U8, name="top1", offset=0, align_bytes=64)
+        gather_top_rows(top1, 1)
+        deal_top_rows(top1, 1)
+        wi_codes = held.tile([P, N // 2], I32, name="wi_codes", align_bytes=64)
+        nc.sync.dma_start(wi_codes[:], wi_words[0].bitcast(I32))
 
         grouped, codes, code_scales = {}, {}, {}
         for sign in (-1, 1):
@@ -94,13 +108,10 @@ def tile_list_cpxtab_hl_crelu_kernel(
 
         def quantise(sign, slot):
             codes[sign] = held.tile([P, 2 * N], U32, name=f"codes{sign + 1}", tag=slot, align_bytes=64)
-            if sign < 0:
-                code_scales[sign] = held.tile([P, 2 * N], U8, name="neg_scales", align_bytes=64)[:]
-            else:
-                code_scales[sign] = shared_plane[4:P, :].bitcast(U8)
+            code_scales[sign] = held.tile([P, 2 * N], U8, name=f"code_scales{sign + 1}", align_bytes=64)
             nc.vector.quantize_mx(
                 out=codes[sign][:].bitcast(FP8X4),
-                scales=code_scales[sign],
+                scales=code_scales[sign][:],
                 in_=grouped[sign][:].rearrange("p h n j -> p (h n j)"),
             )
 
@@ -115,18 +126,17 @@ def tile_list_cpxtab_hl_crelu_kernel(
             )
 
         sc, wd = {}, {}
+        for s in range(SLICES):
+            sc[0, s] = planes[s // 2][:, s % 2 * W // 4 : (s % 2 + 1) * W // 4].bitcast(U8)
 
-        def picks(s):
-            return offsets[:, s * (W // 16) : (s + 1) * (W // 16)]
-
-        def gather_scales(x, s, slot):
-            got = held.tile([P, W], U8, name=f"sc{x}_{s}", tag=slot, align_bytes=64)
-            nc.vector.tensor_copy(got[:], scale_win[x][:].bitcast(U8).indirect(picks(s)))
-            sc[x, s] = got[:]
+        def gather_scales(s, slot):
+            got = held.tile([P, W], U8, name=f"sc1_{s}", tag=slot, align_bytes=64)
+            nc.vector.tensor_copy(got[:], scale_win[1][:].bitcast(U8).indirect(picks(s * W, W)))
+            sc[1, s] = got[:]
 
         def gather_words(x, s, slot):
             got = held.tile([P, W], U32, name=f"wd{x}_{s}", tag=slot, align_bytes=64)
-            nc.vector.tensor_copy(got[:], word_win[x][:].bitcast(U32).indirect(picks(s)))
+            nc.vector.tensor_copy(got[:], word_win[x][:].bitcast(U32).indirect(picks(s * W, W)))
             wd[x, s] = got
 
         def operand(x, s):
@@ -156,8 +166,7 @@ def tile_list_cpxtab_hl_crelu_kernel(
         def open_im(s, pair):
             for h in range(HALVES):
                 im[s, h] = psum.tile([M, W], F32, name=f"im{s}_{h}", tag=f"bank{pair}_{h}")
-                low = low_plane[:, s * W // 4 : (s + 1) * W // 4].bitcast(U8)
-                mm(im[s, h], wi_part(h), (operand(0, s)[0], low), True, False)
+                mm(im[s, h], wi_part(h), operand(0, s), True, False)
 
         def close_re(s):
             for h in range(HALVES):
@@ -170,40 +179,30 @@ def tile_list_cpxtab_hl_crelu_kernel(
                 mm(im[s, h], wr_part(1, 1, h), operand(1, s), False, True)
                 finish(im[s, h], 1.0, out_1, h, s, s == SLICES - 1 and h == 1)
 
-        sc_all = held.tile([P, J], U8, name="sc_all", align_bytes=64)
-        nc.vector.tensor_copy(sc_all[:], scale_win[0][:].bitcast(U8).indirect(offsets[:]))
-        for s in range(SLICES):
-            sc[0, s] = sc_all[4:P, s * W : (s + 1) * W]
-        for r in range(4):
-            nc.sync.dma_start(low_plane[r:P:32, :], sc_all[4 + r : P : 32, :].bitcast(I32))
-        wi_codes = held.tile([P, N // 2], I32, name="wi_codes", align_bytes=64)
-        nc.sync.dma_start(wi_codes[:], wi_words[0].bitcast(I32))
-        quantise(-1, "scale_win0")
-        for s in range(2):
+        gather_scales(0, "slot3")
+        quantise(-1, "codes_neg")
+        for s in range(3):
             gather_words(0, s, f"slot{s}")
             open_re(s, s)
-        gather_scales(1, 0, "slot3")
-        quantise(1, "codes_pos")
-        open_im(0, 2)
+        quantise(1, "top0")
+        open_im(0, 3)
         gather_words(1, 0, "slot4")
         close_re(0)
         close_im(0)
-        open_im(1, 3)
+        open_im(1, 0)
         gather_words(1, 1, "slot5")
-        gather_scales(1, 1, "slot0")
+        gather_scales(1, "slot0")
         close_re(1)
         close_im(1)
-        gather_words(0, 2, "slot4")
-        open_re(2, 0)
-        open_im(2, 2)
-        gather_words(1, 2, "slot3")
-        gather_scales(1, 2, "slot1")
+        open_im(2, 3)
+        gather_words(1, 2, "slot4")
+        gather_scales(2, "slot1")
         close_re(2)
         close_im(2)
         gather_words(0, 3, "slot5")
         open_re(3, 1)
-        open_im(3, 3)
-        gather_scales(1, 3, "slot0")
+        open_im(3, 0)
+        gather_scales(3, "slot2")
         gather_words(1, 3, "slot4")
         close_re(3)
         close_im(3)

@@ -1,6 +1,7 @@
 from contextlib import ExitStack
 
 import concourse.mybir as mybir
+from concourse.masks import make_identity
 
 K, N, T, J = 512, 256, 4096, 2048
 FLOPS = 6 * 2 * K * N * J
@@ -25,6 +26,10 @@ SLICES = J // W
 ROWS = 16
 TOP = P - ROWS
 HI_MASK = -(1 << 20)
+SIGN_BIT = -(1 << 31)
+AT_TOP0 = 4096
+AT_TURNED = 5120
+AT_NEG_LO = 9216
 
 
 def tile_list_cpxtab_hl_crelu_kernel(
@@ -44,7 +49,7 @@ def tile_list_cpxtab_hl_crelu_kernel(
         nc.vector.memset(scale_win[1][:], 0)
         nc.vector.memset(scale_win[0][:TOP], 0)
         nc.sync.dma_start(scale_win[0][TOP:], tab_scales[0].bitcast(I32))
-        raw = reused.tile([P, PACK, N], F32, name="raw", offset=0, align_bytes=64)
+        raw = held.tile([P, PACK, N], F32, name="raw")
         nc.sync.dma_start(raw[:], wr.rearrange("(p j) n -> p j n", j=PACK))
         for r in range(4):
             nc.sync.dma_start(scale_win[1][r:P:32, :], tab2_scales[0, r:16:4, :].bitcast(I32))
@@ -52,6 +57,8 @@ def tile_list_cpxtab_hl_crelu_kernel(
         for plane in planes:
             nc.vector.memset(plane[:], 0)
 
+        ident = held.tile([P, P], F32, name="ident")
+        make_identity(nc, ident[:])
         wi_plane = held.tile([P, N // 4], I32, name="wi_plane", align_bytes=64)
         nc.gpsimd.memset(wi_plane[:], 0)
         for r in range(4):
@@ -73,51 +80,90 @@ def tile_list_cpxtab_hl_crelu_kernel(
             for r in range(4):
                 nc.sync.dma_start(planes[half][r:P:32, :], got[TOP + r : P : 4, :].bitcast(I32))
 
-        top0 = held.tile([P, J // 2], U8, name="top0", tag="top0", align_bytes=64)
+        top0 = reused.tile([P, J // 2], U8, name="top0", offset=AT_TOP0, align_bytes=64)
         gather_top_rows(top0, 0)
         deal_top_rows(top0, 0)
 
-        parts = held.tile([P, 2, PACK, N], F32, name="parts")
+        hi_mask = reused.tile([P, 1], I32, name="hi_mask", offset=0, align_bytes=64)
+        nc.gpsimd.memset(hi_mask[:], HI_MASK)
+        neg_hi = held.tile([P, PACK, N], F32, name="neg_hi")
         nc.vector.tensor_scalar(
-            out=parts[:, 0].bitcast(I32),
+            out=neg_hi[:].bitcast(I32),
             in0=raw[:].bitcast(I32),
-            scalar1=HI_MASK,
-            scalar2=None,
+            scalar1=hi_mask[:],
+            scalar2=SIGN_BIT,
             op0=ALU.bitwise_and,
+            op1=ALU.bitwise_xor,
         )
-        nc.vector.tensor_tensor(out=parts[:, 1], in0=raw[:], in1=parts[:, 0], op=ALU.subtract)
 
         word_win.append(held.tile([P, T], I32, name="word_win1", align_bytes=64))
         load_words(word_win[1], tab2_words)
+
+        grouped, codes, code_scales = {}, {}, {}
+
+        def lay_hi(sign):
+            nc.scalar.activation(
+                out=grouped[sign, 0], in_=neg_hi[:].rearrange("p j n -> p n j"), func=ACT.Copy, scale=float(-sign)
+            )
+
+        def lay_lo(sign):
+            for h in range(HALVES):
+                nc.scalar.activation(
+                    out=grouped[sign, 1][:, h * M : (h + 1) * M],
+                    in_=lo[h][:].rearrange("p j n -> p n j"),
+                    func=ACT.Copy,
+                    scale=float(sign),
+                )
+
+        grouped[-1, 0] = held.tile([P, N, PACK], BF16, name="neg_hi_grouped", align_bytes=64)[:]
+        lay_hi(-1)
+        turned = [psum.tile([M, PACK, P], F32, name=f"turned{h}", tag=f"bank2_{h}") for h in range(HALVES)]
+        for term, source in enumerate((raw, neg_hi)):
+            for h in range(HALVES):
+                for j in range(PACK):
+                    nc.tensor.matmul(
+                        turned[h][:, j],
+                        source[:, j, h * M : (h + 1) * M],
+                        ident[:],
+                        start=term == 0 and j == 0,
+                        stop=term == 1 and j == PACK - 1,
+                        is_transpose=True,
+                    )
+        lo = []
+        for h in range(HALVES):
+            lo_turned = reused.tile([M, PACK, P], F32, name=f"lo_turned{h}", offset=AT_TURNED + 2048 * h, align_bytes=64)
+            nc.scalar.copy(lo_turned[:], turned[h][:])
+            lo.append(psum.tile([P, PACK, M], F32, name=f"lo{h}", tag=f"bank3_{h}"))
+            for j in range(PACK):
+                nc.tensor.transpose(lo[h][:, j], lo_turned[:, j], ident[:])
+        grouped[-1, 1] = reused.tile([P, N, PACK], BF16, name="neg_lo_grouped", offset=AT_NEG_LO, align_bytes=64)[:]
+        lay_lo(-1)
+        pos_grouped = reused.tile([P, 2, N, PACK], BF16, name="pos_grouped", offset=AT_TURNED, align_bytes=64)
+        grouped[1, 0], grouped[1, 1] = pos_grouped[:, 0], pos_grouped[:, 1]
+        lay_hi(1)
+        lay_lo(1)
+
         top1 = reused.tile([P, J // 2], U8, name="top1", offset=0, align_bytes=64)
         gather_top_rows(top1, 1)
         deal_top_rows(top1, 1)
         wi_codes = held.tile([P, N // 2], I32, name="wi_codes", align_bytes=64)
         nc.sync.dma_start(wi_codes[:], wi_words[0].bitcast(I32))
 
-        grouped, codes, code_scales = {}, {}, {}
-        for sign in (-1, 1):
-            grouped[sign] = held.tile([P, 2, N, PACK], BF16, name=f"grouped{sign + 1}", align_bytes=64)
-            for h in range(2):
-                nc.scalar.activation(
-                    out=grouped[sign][:, h],
-                    in_=parts[:, h].rearrange("p j n -> p n j"),
-                    func=ACT.Copy,
-                    scale=float(sign),
-                )
-
-        def quantise(sign, slot):
-            codes[sign] = held.tile([P, 2 * N], U32, name=f"codes{sign + 1}", tag=slot, align_bytes=64)
-            code_scales[sign] = held.tile([P, 2 * N], U8, name=f"code_scales{sign + 1}", align_bytes=64)
-            nc.vector.quantize_mx(
-                out=codes[sign][:].bitcast(FP8X4),
-                scales=code_scales[sign][:],
-                in_=grouped[sign][:].rearrange("p h n j -> p (h n j)"),
-            )
+        def quantise(name, values, keys, at):
+            width = N * len(keys)
+            words = held.tile([P, width], U32, name=f"{name}_codes", align_bytes=64)
+            if at is None:
+                scales = held.tile([P, width], U8, name=f"{name}_scales", align_bytes=64)
+            else:
+                scales = reused.tile([P, width], U8, name=f"{name}_scales", offset=at, align_bytes=64)
+            nc.vector.quantize_mx(out=words[:].bitcast(FP8X4), scales=scales[:], in_=values)
+            for place, key in enumerate(keys):
+                codes[key] = words[:, place * N : (place + 1) * N]
+                code_scales[key] = scales[:, place * N : (place + 1) * N]
 
         def wr_part(sign, part, half):
-            cols = slice(part * N + half * M, part * N + (half + 1) * M)
-            return codes[sign][:, cols].bitcast(FP8X4), code_scales[sign][:, cols]
+            cols = slice(half * M, (half + 1) * M)
+            return codes[sign, part][:, cols].bitcast(FP8X4), code_scales[sign, part][:, cols]
 
         def wi_part(half):
             return (
@@ -130,12 +176,18 @@ def tile_list_cpxtab_hl_crelu_kernel(
             sc[0, s] = planes[s // 2][:, s % 2 * W // 4 : (s % 2 + 1) * W // 4].bitcast(U8)
 
         def gather_scales(s, slot):
-            got = held.tile([P, W], U8, name=f"sc1_{s}", tag=slot, align_bytes=64)
+            if slot == "slot2":
+                got = reused.tile([P, W], U8, name=f"sc1_{s}", offset=AT_NEG_LO, align_bytes=64)
+            else:
+                got = held.tile([P, W], U8, name=f"sc1_{s}", tag=slot, align_bytes=64)
             nc.vector.tensor_copy(got[:], scale_win[1][:].bitcast(U8).indirect(picks(s * W, W)))
             sc[1, s] = got[:]
 
         def gather_words(x, s, slot):
-            got = held.tile([P, W], U32, name=f"wd{x}_{s}", tag=slot, align_bytes=64)
+            if slot == "slot2":
+                got = reused.tile([P, W], U32, name=f"wd{x}_{s}", offset=AT_NEG_LO, align_bytes=64)
+            else:
+                got = held.tile([P, W], U32, name=f"wd{x}_{s}", tag=slot, align_bytes=64)
             nc.vector.tensor_copy(got[:], word_win[x][:].bitcast(U32).indirect(picks(s * W, W)))
             wd[x, s] = got
 
@@ -161,6 +213,9 @@ def tile_list_cpxtab_hl_crelu_kernel(
             for h in range(HALVES):
                 re[s, h] = psum.tile([M, W], F32, name=f"re{s}_{h}", tag=f"bank{pair}_{h}")
                 mm(re[s, h], wr_part(-1, 0, h), operand(0, s), True, False)
+
+        def add_re(s):
+            for h in range(HALVES):
                 mm(re[s, h], wr_part(-1, 1, h), operand(0, s), False, False)
 
         def open_im(s, pair):
@@ -180,11 +235,17 @@ def tile_list_cpxtab_hl_crelu_kernel(
                 finish(im[s, h], 1.0, out_1, h, s, s == SLICES - 1 and h == 1)
 
         gather_scales(0, "slot3")
-        quantise(-1, "codes_neg")
-        for s in range(3):
+        quantise("neg_hi", grouped[-1, 0].rearrange("p n j -> p (n j)"), [(-1, 0)], None)
+        for s in range(2):
             gather_words(0, s, f"slot{s}")
             open_re(s, s)
-        quantise(1, "top0")
+        quantise("neg_lo", grouped[-1, 1].rearrange("p n j -> p (n j)"), [(-1, 1)], AT_TOP0)
+        add_re(0)
+        add_re(1)
+        gather_words(0, 2, "slot2")
+        open_re(2, 2)
+        add_re(2)
+        quantise("pos", pos_grouped[:].rearrange("p h n j -> p (h n j)"), [(1, 0), (1, 1)], AT_TOP0 + N)
         open_im(0, 3)
         gather_words(1, 0, "slot4")
         close_re(0)
@@ -201,6 +262,7 @@ def tile_list_cpxtab_hl_crelu_kernel(
         close_im(2)
         gather_words(0, 3, "slot5")
         open_re(3, 1)
+        add_re(3)
         open_im(3, 0)
         gather_scales(3, "slot2")
         gather_words(1, 3, "slot4")

@@ -48,12 +48,13 @@ def tile_list_cpxtab_hl_crelu_kernel(
         scale_win = [held.tile([P, T // 4], I32, name=f"scale_win{x}", align_bytes=64) for x in range(2)]
         nc.vector.memset(scale_win[1][:], 0)
         nc.vector.memset(scale_win[0][:TOP], 0)
-        nc.sync.dma_start(scale_win[0][TOP:], tab_scales[0].bitcast(I32))
+        nc.scalar.dma_start(scale_win[0][TOP:], tab_scales[0].bitcast(I32))
         raw = held.tile([P, PACK, N], F32, name="raw")
         nc.sync.dma_start(raw[:], wr.rearrange("(p j) n -> p j n", j=PACK))
         for r in range(4):
             nc.sync.dma_start(scale_win[1][r:P:32, :], tab2_scales[0, r:16:4, :].bitcast(I32))
-        planes = [held.tile([P, J // 8], I32, name=f"plane{half}", align_bytes=64) for half in range(2)]
+        widths = [2 * W, W, W]
+        planes = [held.tile([P, widths[run] // 4], I32, name=f"plane{run}", align_bytes=64) for run in range(3)]
         for plane in planes:
             nc.vector.memset(plane[:], 0)
 
@@ -64,11 +65,11 @@ def tile_list_cpxtab_hl_crelu_kernel(
         for r in range(4):
             nc.gpsimd.dma_start(wi_plane[r:P:32, :], wi_scales[0, r:16:4, :].bitcast(I32))
 
-        def load_words(win, words):
-            nc.sync.dma_start(win[:], words[0].rearrange("p t i -> p (t i)").bitcast(I32))
+        def load_words(win, words, cols):
+            nc.sync.dma_start(win[:, cols], words[0].rearrange("p t i -> p (t i)").bitcast(I32)[:, cols])
 
         word_win = [held.tile([P, T], I32, name="word_win0", align_bytes=64)]
-        load_words(word_win[0], tab_words)
+        load_words(word_win[0], tab_words, slice(0, T))
 
         def picks(first, count):
             return offsets[:, first // 16 : (first + count) // 16]
@@ -76,13 +77,13 @@ def tile_list_cpxtab_hl_crelu_kernel(
         def gather_top_rows(got, half):
             nc.vector.tensor_copy(got[:], scale_win[0][:].bitcast(U8).indirect(picks(half * J // 2, J // 2)))
 
-        def deal_top_rows(got, half):
+        def deal_top_rows(got, plane, queue):
             for r in range(4):
-                nc.sync.dma_start(planes[half][r:P:32, :], got[TOP + r : P : 4, :].bitcast(I32))
+                queue.dma_start(plane[r:P:32, :], got[TOP + r : P : 4].bitcast(I32))
 
         top0 = reused.tile([P, J // 2], U8, name="top0", offset=AT_TOP0, align_bytes=64)
         gather_top_rows(top0, 0)
-        deal_top_rows(top0, 0)
+        deal_top_rows(top0[:], planes[0], nc.sync)
 
         hi_mask = reused.tile([P, 1], I32, name="hi_mask", offset=0, align_bytes=64)
         nc.gpsimd.memset(hi_mask[:], HI_MASK)
@@ -97,7 +98,7 @@ def tile_list_cpxtab_hl_crelu_kernel(
         )
 
         word_win.append(held.tile([P, T], I32, name="word_win1", align_bytes=64))
-        load_words(word_win[1], tab2_words)
+        load_words(word_win[1], tab2_words, slice(0, T // 2))
 
         grouped, codes, code_scales = {}, {}, {}
 
@@ -145,7 +146,9 @@ def tile_list_cpxtab_hl_crelu_kernel(
 
         top1 = reused.tile([P, J // 2], U8, name="top1", offset=0, align_bytes=64)
         gather_top_rows(top1, 1)
-        deal_top_rows(top1, 1)
+        deal_top_rows(top1[:, :W], planes[1], nc.sync)
+        load_words(word_win[1], tab2_words, slice(T // 2, T))
+        deal_top_rows(top1[:, W:], planes[2], nc.sync)
         wi_codes = held.tile([P, N // 2], I32, name="wi_codes", align_bytes=64)
         nc.sync.dma_start(wi_codes[:], wi_words[0].bitcast(I32))
 
@@ -172,12 +175,13 @@ def tile_list_cpxtab_hl_crelu_kernel(
             )
 
         sc, wd = {}, {}
-        for s in range(SLICES):
-            sc[0, s] = planes[s // 2][:, s % 2 * W // 4 : (s % 2 + 1) * W // 4].bitcast(U8)
+        for s in range(2):
+            sc[0, s] = planes[0][:, s * W // 4 : (s + 1) * W // 4].bitcast(U8)
+            sc[0, 2 + s] = planes[1 + s][:].bitcast(U8)
 
         def gather_scales(s, slot):
-            if slot == "slot2":
-                got = reused.tile([P, W], U8, name=f"sc1_{s}", offset=AT_NEG_LO, align_bytes=64)
+            if slot in (AT_NEG_LO, 0):
+                got = reused.tile([P, W], U8, name=f"sc1_{s}", offset=slot, align_bytes=64)
             else:
                 got = held.tile([P, W], U8, name=f"sc1_{s}", tag=slot, align_bytes=64)
             nc.vector.tensor_copy(got[:], scale_win[1][:].bitcast(U8).indirect(picks(s * W, W)))
@@ -264,7 +268,7 @@ def tile_list_cpxtab_hl_crelu_kernel(
         open_re(3, 1)
         add_re(3)
         open_im(3, 0)
-        gather_scales(3, "slot2")
+        gather_scales(3, AT_NEG_LO)
         gather_words(1, 3, "slot4")
         close_re(3)
         close_im(3)

@@ -53,8 +53,7 @@ def tile_list_cpxtab_hl_crelu_kernel(
         nc.sync.dma_start(raw[:], wr.rearrange("(p j) n -> p j n", j=PACK))
         for r in range(4):
             nc.sync.dma_start(scale_win[1][r:P:32, :], tab2_scales[0, r:16:4, :].bitcast(I32))
-        widths = [2 * W, W, W]
-        planes = [held.tile([P, widths[run] // 4], I32, name=f"plane{run}", align_bytes=64) for run in range(3)]
+        planes = [held.tile([P, J // 8], I32, name=f"plane{half}", align_bytes=64) for half in range(2)]
         for plane in planes:
             nc.vector.memset(plane[:], 0)
 
@@ -62,8 +61,6 @@ def tile_list_cpxtab_hl_crelu_kernel(
         make_identity(nc, ident[:])
         wi_plane = held.tile([P, N // 4], I32, name="wi_plane", align_bytes=64)
         nc.gpsimd.memset(wi_plane[:], 0)
-        for r in range(4):
-            nc.gpsimd.dma_start(wi_plane[r:P:32, :], wi_scales[0, r:16:4, :].bitcast(I32))
 
         def load_words(win, words, cols):
             nc.sync.dma_start(win[:, cols], words[0].rearrange("p t i -> p (t i)").bitcast(I32)[:, cols])
@@ -146,11 +143,12 @@ def tile_list_cpxtab_hl_crelu_kernel(
 
         top1 = reused.tile([P, J // 2], U8, name="top1", offset=0, align_bytes=64)
         gather_top_rows(top1, 1)
-        deal_top_rows(top1[:, :W], planes[1], nc.sync)
-        load_words(word_win[1], tab2_words, slice(T // 2, T))
-        deal_top_rows(top1[:, W:], planes[2], nc.sync)
+        deal_top_rows(top1[:], planes[1], nc.sync)
         wi_codes = held.tile([P, N // 2], I32, name="wi_codes", align_bytes=64)
         nc.sync.dma_start(wi_codes[:], wi_words[0].bitcast(I32))
+        load_words(word_win[1], tab2_words, slice(T // 2, T))
+        for r in range(4):
+            nc.sync.dma_start(wi_plane[r:P:32, :], wi_scales[0, r:16:4, :].bitcast(I32))
 
         def quantise(name, values, keys, at):
             width = N * len(keys)
@@ -175,9 +173,8 @@ def tile_list_cpxtab_hl_crelu_kernel(
             )
 
         sc, wd = {}, {}
-        for s in range(2):
-            sc[0, s] = planes[0][:, s * W // 4 : (s + 1) * W // 4].bitcast(U8)
-            sc[0, 2 + s] = planes[1 + s][:].bitcast(U8)
+        for s in range(SLICES):
+            sc[0, s] = planes[s // 2][:, s % 2 * W // 4 : (s % 2 + 1) * W // 4].bitcast(U8)
 
         def gather_scales(s, slot):
             if slot in (AT_NEG_LO, 0):

@@ -51,7 +51,7 @@ def tile_list_cpxtab_hl_crelu_kernel(
         nc.scalar.dma_start(scale_win[0][TOP:], tab_scales[0].bitcast(I32))
         raw = held.tile([P, PACK, N], F32, name="raw")
         nc.sync.dma_start(raw[:], wr.rearrange("(p j) n -> p j n", j=PACK))
-        for r in range(4):
+        for r in range(2):
             nc.sync.dma_start(scale_win[1][r:P:32, :], tab2_scales[0, r:16:4, :].bitcast(I32))
         planes = [held.tile([P, J // 8], I32, name=f"plane{half}", align_bytes=64) for half in range(2)]
         for plane in planes:
@@ -67,6 +67,8 @@ def tile_list_cpxtab_hl_crelu_kernel(
 
         word_win = [held.tile([P, T], I32, name="word_win0", align_bytes=64)]
         load_words(word_win[0], tab_words, slice(0, T))
+        for r in range(2, 4):
+            nc.sync.dma_start(scale_win[1][r:P:32, :], tab2_scales[0, r:16:4, :].bitcast(I32))
 
         def picks(first, count):
             return offsets[:, first // 16 : (first + count) // 16]
@@ -177,7 +179,7 @@ def tile_list_cpxtab_hl_crelu_kernel(
             sc[0, s] = planes[s // 2][:, s % 2 * W // 4 : (s % 2 + 1) * W // 4].bitcast(U8)
 
         def gather_scales(s, slot):
-            if slot in (AT_NEG_LO, 0):
+            if slot == AT_NEG_LO + W:
                 got = reused.tile([P, W], U8, name=f"sc1_{s}", offset=slot, align_bytes=64)
             else:
                 got = held.tile([P, W], U8, name=f"sc1_{s}", tag=slot, align_bytes=64)
@@ -186,7 +188,7 @@ def tile_list_cpxtab_hl_crelu_kernel(
 
         def gather_words(x, s, slot):
             if slot == "slot2":
-                got = reused.tile([P, W], U32, name=f"wd{x}_{s}", offset=AT_NEG_LO, align_bytes=64)
+                got = reused.tile([P, W], U32, name=f"wd{x}_{s}", offset=AT_NEG_LO + W, align_bytes=64)
             else:
                 got = held.tile([P, W], U32, name=f"wd{x}_{s}", tag=slot, align_bytes=64)
             nc.vector.tensor_copy(got[:], word_win[x][:].bitcast(U32).indirect(picks(s * W, W)))
@@ -235,7 +237,6 @@ def tile_list_cpxtab_hl_crelu_kernel(
                 mm(im[s, h], wr_part(1, 1, h), operand(1, s), False, True)
                 finish(im[s, h], 1.0, out_1, h, s, s == SLICES - 1 and h == 1)
 
-        gather_scales(0, "slot3")
         quantise("neg_hi", grouped[-1, 0].rearrange("p n j -> p (n j)"), [(-1, 0)], None)
         for s in range(2):
             gather_words(0, s, f"slot{s}")
@@ -246,7 +247,8 @@ def tile_list_cpxtab_hl_crelu_kernel(
         gather_words(0, 2, "slot2")
         open_re(2, 2)
         add_re(2)
-        quantise("pos", pos_grouped[:].rearrange("p h n j -> p (h n j)"), [(1, 0), (1, 1)], AT_TOP0 + N)
+        gather_scales(0, "slot3")
+        quantise("pos", pos_grouped[:].rearrange("p h n j -> p (h n j)"), [(1, 0), (1, 1)], AT_NEG_LO)
         open_im(0, 3)
         gather_words(1, 0, "slot4")
         close_re(0)
@@ -265,7 +267,7 @@ def tile_list_cpxtab_hl_crelu_kernel(
         open_re(3, 1)
         add_re(3)
         open_im(3, 0)
-        gather_scales(3, AT_NEG_LO)
+        gather_scales(3, AT_NEG_LO + W)
         gather_words(1, 3, "slot4")
         close_re(3)
         close_im(3)

@@ -27,9 +27,10 @@ ROWS = 16
 TOP = P - ROWS
 HI_MASK = -(1 << 20)
 SIGN_BIT = -(1 << 31)
-AT_TOP0 = 4096
-AT_TURNED = 5120
-AT_NEG_LO = 9216
+AT_TOP1 = 2048
+AT_TOP0 = 7168
+AT_TURNED = 8192
+AT_NEG_LO = 12288
 
 
 def tile_list_cpxtab_hl_crelu_kernel(
@@ -51,24 +52,25 @@ def tile_list_cpxtab_hl_crelu_kernel(
         nc.scalar.dma_start(scale_win[0][TOP:], tab_scales[0].bitcast(I32))
         raw = held.tile([P, PACK, N], F32, name="raw")
         nc.sync.dma_start(raw[:], wr.rearrange("(p j) n -> p j n", j=PACK))
-        for r in range(2):
-            nc.sync.dma_start(scale_win[1][r:P:32, :], tab2_scales[0, r:16:4, :].bitcast(I32))
-        planes = [held.tile([P, J // 8], I32, name=f"plane{half}", align_bytes=64) for half in range(2)]
+        nc.sync.dma_start(scale_win[1][4:P:8, :], tab2_scales[0].bitcast(I32))
+        planes = [
+            held.tile([P, width // 4], I32, name=f"plane{c}", align_bytes=64)[:] for c, width in enumerate((2 * W, W, W, W))
+        ]
         for plane in planes:
-            nc.vector.memset(plane[:], 0)
+            nc.vector.memset(plane, 0)
 
         ident = held.tile([P, P], F32, name="ident")
         make_identity(nc, ident[:])
         wi_plane = held.tile([P, N // 4], I32, name="wi_plane", align_bytes=64)
         nc.gpsimd.memset(wi_plane[:], 0)
+        for r in range(4):
+            nc.sync.dma_start(wi_plane[r:P:32, :], wi_scales[0, r:16:4, :].bitcast(I32))
 
         def load_words(win, words, cols):
             nc.sync.dma_start(win[:, cols], words[0].rearrange("p t i -> p (t i)").bitcast(I32)[:, cols])
 
         word_win = [held.tile([P, T], I32, name="word_win0", align_bytes=64)]
         load_words(word_win[0], tab_words, slice(0, T))
-        for r in range(2, 4):
-            nc.sync.dma_start(scale_win[1][r:P:32, :], tab2_scales[0, r:16:4, :].bitcast(I32))
 
         def picks(first, count):
             return offsets[:, first // 16 : (first + count) // 16]
@@ -84,7 +86,7 @@ def tile_list_cpxtab_hl_crelu_kernel(
         gather_top_rows(top0, 0)
         deal_top_rows(top0[:], planes[0], nc.sync)
 
-        hi_mask = reused.tile([P, 1], I32, name="hi_mask", offset=0, align_bytes=64)
+        hi_mask = reused.tile([P, 1], I32, name="hi_mask", offset=AT_TOP1, align_bytes=64)
         nc.gpsimd.memset(hi_mask[:], HI_MASK)
         neg_hi = held.tile([P, PACK, N], F32, name="neg_hi")
         nc.vector.tensor_scalar(
@@ -143,14 +145,12 @@ def tile_list_cpxtab_hl_crelu_kernel(
         lay_hi(1)
         lay_lo(1)
 
-        top1 = reused.tile([P, J // 2], U8, name="top1", offset=0, align_bytes=64)
+        top1 = reused.tile([P, J // 2], U8, name="top1", offset=AT_TOP1, align_bytes=64)
         gather_top_rows(top1, 1)
-        deal_top_rows(top1[:], planes[1], nc.sync)
+        deal_top_rows(top1[:, :W], planes[1], nc.sync)
         wi_codes = held.tile([P, N // 2], I32, name="wi_codes", align_bytes=64)
         nc.sync.dma_start(wi_codes[:], wi_words[0].bitcast(I32))
         load_words(word_win[1], tab2_words, slice(T // 2, T))
-        for r in range(4):
-            nc.sync.dma_start(wi_plane[r:P:32, :], wi_scales[0, r:16:4, :].bitcast(I32))
 
         def quantise(name, values, keys, at):
             width = N * len(keys)
@@ -175,11 +175,12 @@ def tile_list_cpxtab_hl_crelu_kernel(
             )
 
         sc, wd = {}, {}
-        for s in range(SLICES):
-            sc[0, s] = planes[s // 2][:, s % 2 * W // 4 : (s % 2 + 1) * W // 4].bitcast(U8)
+        for s in range(2):
+            sc[0, s] = planes[0][:, s * W // 4 : (s + 1) * W // 4].bitcast(U8)
+        sc[0, 2], sc[0, 3] = planes[1].bitcast(U8), planes[3].bitcast(U8)
 
         def gather_scales(s, slot):
-            if slot == AT_NEG_LO + W:
+            if isinstance(slot, int):
                 got = reused.tile([P, W], U8, name=f"sc1_{s}", offset=slot, align_bytes=64)
             else:
                 got = held.tile([P, W], U8, name=f"sc1_{s}", tag=slot, align_bytes=64)
@@ -187,15 +188,17 @@ def tile_list_cpxtab_hl_crelu_kernel(
             sc[1, s] = got[:]
 
         def gather_words(x, s, slot):
-            if slot == "slot2":
-                got = reused.tile([P, W], U32, name=f"wd{x}_{s}", offset=AT_NEG_LO + W, align_bytes=64)
+            if isinstance(slot, int):
+                got = reused.tile([P, W], U32, name=f"wd{x}_{s}", offset=slot, align_bytes=64)[:]
+            elif isinstance(slot, str):
+                got = held.tile([P, W], U32, name=f"wd{x}_{s}", tag=slot, align_bytes=64)[:]
             else:
-                got = held.tile([P, W], U32, name=f"wd{x}_{s}", tag=slot, align_bytes=64)
-            nc.vector.tensor_copy(got[:], word_win[x][:].bitcast(U32).indirect(picks(s * W, W)))
+                got = slot
+            nc.vector.tensor_copy(got, word_win[x][:].bitcast(U32).indirect(picks(s * W, W)))
             wd[x, s] = got
 
         def operand(x, s):
-            return wd[x, s][:].bitcast(FP8X4), sc[x, s]
+            return wd[x, s].bitcast(FP8X4), sc[x, s]
 
         def mm(acc, lhs, rhs, start, stop):
             nc.tensor.matmul_mx(
@@ -244,10 +247,16 @@ def tile_list_cpxtab_hl_crelu_kernel(
         quantise("neg_lo", grouped[-1, 1].rearrange("p n j -> p (n j)"), [(-1, 1)], AT_TOP0)
         add_re(0)
         add_re(1)
-        gather_words(0, 2, "slot2")
+        gather_scales(0, AT_TOP0 + W)
+        for r in range(4):
+            nc.sync.dma_start(planes[2][r:P:32, :], sc[1, 0][4 + 8 * r : P : 32].bitcast(I32))
+        sc[1, 0] = planes[2].bitcast(U8)
+        for r in range(4):
+            nc.sync.dma_start(scale_win[1][r:P:32, :], tab2_scales[0, r:16:4, :].bitcast(I32))
+        deal_top_rows(top1[:, W:], planes[3], nc.sync)
+        gather_words(0, 2, AT_NEG_LO + W)
         open_re(2, 2)
         add_re(2)
-        gather_scales(0, "slot3")
         quantise("pos", pos_grouped[:].rearrange("p h n j -> p (h n j)"), [(1, 0), (1, 1)], AT_NEG_LO)
         open_im(0, 3)
         gather_words(1, 0, "slot4")
@@ -255,19 +264,20 @@ def tile_list_cpxtab_hl_crelu_kernel(
         close_im(0)
         open_im(1, 0)
         gather_words(1, 1, "slot5")
-        gather_scales(1, "slot0")
+        gather_scales(1, "second1")
         close_re(1)
         close_im(1)
         open_im(2, 3)
-        gather_words(1, 2, "slot4")
-        gather_scales(2, "slot1")
+        gather_words(1, 2, AT_TOP1 + 256 - 4 * W)
+        gather_scales(2, "second2")
         close_re(2)
         close_im(2)
-        gather_words(0, 3, "slot5")
+        last = reused.tile([P, 2 * W], U32, name="last_words", offset=AT_TOP1 + 256 + W, align_bytes=64)
+        gather_words(0, 3, last[:, :W])
         open_re(3, 1)
         add_re(3)
         open_im(3, 0)
-        gather_scales(3, AT_NEG_LO + W)
-        gather_words(1, 3, "slot4")
+        gather_scales(3, AT_TOP1 + 256)
+        gather_words(1, 3, last[:, W:])
         close_re(3)
         close_im(3)

@@ -46,13 +46,14 @@ def tile_list_cpxtab_hl_crelu_kernel(
         offsets = held.tile([P, J // 16], U16, name="offsets")
         nc.sync.dma_start(offsets[:], offs)
 
+        wi_plane = held.tile([P, N // 4], I32, name="wi_plane", align_bytes=64)
+        nc.vector.memset(wi_plane[:], 0)
         scale_win = [held.tile([P, T // 4], I32, name=f"scale_win{x}", align_bytes=64) for x in range(2)]
         nc.vector.memset(scale_win[1][:], 0)
         nc.vector.memset(scale_win[0][:TOP], 0)
         nc.scalar.dma_start(scale_win[0][TOP:], tab_scales[0].bitcast(I32))
         raw = held.tile([P, PACK, N], F32, name="raw")
         nc.sync.dma_start(raw[:], wr.rearrange("(p j) n -> p j n", j=PACK))
-        nc.sync.dma_start(scale_win[1][4:P:8, :], tab2_scales[0].bitcast(I32))
         planes = [
             held.tile([P, width // 4], I32, name=f"plane{c}", align_bytes=64)[:] for c, width in enumerate((2 * W, W, W, W))
         ]
@@ -61,16 +62,16 @@ def tile_list_cpxtab_hl_crelu_kernel(
 
         ident = held.tile([P, P], F32, name="ident")
         make_identity(nc, ident[:])
-        wi_plane = held.tile([P, N // 4], I32, name="wi_plane", align_bytes=64)
-        nc.gpsimd.memset(wi_plane[:], 0)
-        for r in range(4):
-            nc.sync.dma_start(wi_plane[r:P:32, :], wi_scales[0, r:16:4, :].bitcast(I32))
 
         def load_words(win, words, cols):
             nc.sync.dma_start(win[:, cols], words[0].rearrange("p t i -> p (t i)").bitcast(I32)[:, cols])
 
         word_win = [held.tile([P, T], I32, name="word_win0", align_bytes=64)]
-        load_words(word_win[0], tab_words, slice(0, T))
+        for r in range(4):
+            if r == 3:
+                load_words(word_win[0], tab_words, slice(0, T))
+            nc.sync.dma_start(wi_plane[r:P:32, :], wi_scales[0, r:16:4, :].bitcast(I32))
+        nc.sync.dma_start(scale_win[1][4:P:8, :], tab2_scales[0].bitcast(I32))
 
         def picks(first, count):
             return offsets[:, first // 16 : (first + count) // 16]
@@ -99,7 +100,7 @@ def tile_list_cpxtab_hl_crelu_kernel(
         )
 
         word_win.append(held.tile([P, T], I32, name="word_win1", align_bytes=64))
-        load_words(word_win[1], tab2_words, slice(0, T // 2))
+        load_words(word_win[1], tab2_words, slice(0, 3 * T // 4))
 
         grouped, codes, code_scales = {}, {}, {}
 
@@ -150,7 +151,7 @@ def tile_list_cpxtab_hl_crelu_kernel(
         deal_top_rows(top1[:, :W], planes[1], nc.sync)
         wi_codes = held.tile([P, N // 2], I32, name="wi_codes", align_bytes=64)
         nc.sync.dma_start(wi_codes[:], wi_words[0].bitcast(I32))
-        load_words(word_win[1], tab2_words, slice(T // 2, T))
+        load_words(word_win[1], tab2_words, slice(3 * T // 4, T))
 
         def quantise(name, values, keys, at):
             width = N * len(keys)

@@ -25,8 +25,8 @@ W = 512
 SLICES = J // W
 ROWS = 16
 TOP = P - ROWS
-HI_MASK = -(1 << 20)
-SIGN_BIT = -(1 << 31)
+HI_MASK = -((15 << 16) + 16)
+SIGN_BITS = -(1 << 31) + (1 << 15)
 AT_TOP1 = 2048
 AT_TOP0 = 7168
 AT_TURNED = 8192
@@ -67,10 +67,7 @@ def tile_list_cpxtab_hl_crelu_kernel(
             nc.sync.dma_start(win[:, cols], words[0].rearrange("p t i -> p (t i)").bitcast(I32)[:, cols])
 
         word_win = [held.tile([P, T], I32, name="word_win0", align_bytes=64)]
-        for r in range(4):
-            if r == 3:
-                load_words(word_win[0], tab_words, slice(0, T))
-            nc.sync.dma_start(wi_plane[r:P:32, :], wi_scales[0, r:16:4, :].bitcast(I32))
+        load_words(word_win[0], tab_words, slice(0, T))
         nc.sync.dma_start(scale_win[1][4:P:8, :], tab2_scales[0].bitcast(I32))
 
         def picks(first, count):
@@ -87,27 +84,33 @@ def tile_list_cpxtab_hl_crelu_kernel(
         gather_top_rows(top0, 0)
         deal_top_rows(top0[:], planes[0], nc.sync)
 
-        hi_mask = reused.tile([P, 1], I32, name="hi_mask", offset=AT_TOP1, align_bytes=64)
+        hi_mask = held.tile([P, 1], I32, name="hi_mask")
         nc.gpsimd.memset(hi_mask[:], HI_MASK)
-        neg_hi = held.tile([P, PACK, N], F32, name="neg_hi")
+        upper = reused.tile([P, N, PACK], BF16, name="upper", offset=AT_TOP1, align_bytes=64)
+        nc.scalar.copy(
+            upper[:].rearrange("p (c i) j -> p c j i", i=4),
+            raw[:].bitcast(BF16).rearrange("p j (c i two) -> p c j i two", i=4, two=2)[:, :, :, :, 1],
+        )
+        neg_hi_grouped = held.tile([P, N, PACK], BF16, name="neg_hi_grouped", align_bytes=64)
         nc.vector.tensor_scalar(
-            out=neg_hi[:].bitcast(I32),
-            in0=raw[:].bitcast(I32),
+            out=neg_hi_grouped[:].rearrange("p n j -> p (n j)").bitcast(I32),
+            in0=upper[:].rearrange("p n j -> p (n j)").bitcast(I32),
             scalar1=hi_mask[:],
-            scalar2=SIGN_BIT,
+            scalar2=SIGN_BITS,
             op0=ALU.bitwise_and,
             op1=ALU.bitwise_xor,
+        )
+        neg_hi = held.tile([P, PACK, N], F32, name="neg_hi")
+        nc.scalar.activation(
+            out=neg_hi[:].rearrange("p j (c i) -> p c j i", i=4),
+            in_=neg_hi_grouped[:].rearrange("p (c i) j -> p c j i", i=4),
+            func=ACT.Copy,
         )
 
         word_win.append(held.tile([P, T], I32, name="word_win1", align_bytes=64))
         load_words(word_win[1], tab2_words, slice(0, 3 * T // 4))
 
         grouped, codes, code_scales = {}, {}, {}
-
-        def lay_hi(sign):
-            nc.scalar.activation(
-                out=grouped[sign, 0], in_=neg_hi[:].rearrange("p j n -> p n j"), func=ACT.Copy, scale=float(-sign)
-            )
 
         def lay_lo(sign):
             for h in range(HALVES):
@@ -118,8 +121,7 @@ def tile_list_cpxtab_hl_crelu_kernel(
                     scale=float(sign),
                 )
 
-        grouped[-1, 0] = held.tile([P, N, PACK], BF16, name="neg_hi_grouped", align_bytes=64)[:]
-        lay_hi(-1)
+        grouped[-1, 0] = neg_hi_grouped[:]
         turned = [psum.tile([M, PACK, P], F32, name=f"turned{h}", tag=f"bank2_{h}") for h in range(HALVES)]
         for term, source in enumerate((raw, neg_hi)):
             for h in range(HALVES):
@@ -143,15 +145,18 @@ def tile_list_cpxtab_hl_crelu_kernel(
         lay_lo(-1)
         pos_grouped = reused.tile([P, 2, N, PACK], BF16, name="pos_grouped", offset=AT_TURNED, align_bytes=64)
         grouped[1, 0], grouped[1, 1] = pos_grouped[:, 0], pos_grouped[:, 1]
-        lay_hi(1)
+        nc.scalar.activation(out=grouped[1, 0], in_=grouped[-1, 0], func=ACT.Copy, scale=-1.0)
         lay_lo(1)
 
         top1 = reused.tile([P, J // 2], U8, name="top1", offset=AT_TOP1, align_bytes=64)
         gather_top_rows(top1, 1)
         deal_top_rows(top1[:, :W], planes[1], nc.sync)
+        for r in range(4):
+            if r == 2:
+                load_words(word_win[1], tab2_words, slice(3 * T // 4, T))
+            nc.sync.dma_start(wi_plane[r:P:32, :], wi_scales[0, r:16:4, :].bitcast(I32))
         wi_codes = held.tile([P, N // 2], I32, name="wi_codes", align_bytes=64)
         nc.sync.dma_start(wi_codes[:], wi_words[0].bitcast(I32))
-        load_words(word_win[1], tab2_words, slice(3 * T // 4, T))
 
         def quantise(name, values, keys, at):
             width = N * len(keys)

@@ -40,7 +40,7 @@ def tile_list_cpxtab_hl_crelu_kernel(
     with ExitStack() as ctx:
         held = ctx.enter_context(tc.tile_pool(name="held", bufs=1))
         reused = ctx.enter_context(tc.tile_pool(name="reused", bufs=1))
-        stage = ctx.enter_context(tc.tile_pool(name="stage", bufs=8))
+        stage = ctx.enter_context(tc.tile_pool(name="stage", bufs=17))
         psum = ctx.enter_context(tc.psum_pool(name="psum", bufs=1))
 
         offsets = held.tile([P, J // 16], U16, name="offsets")
@@ -84,28 +84,32 @@ def tile_list_cpxtab_hl_crelu_kernel(
         gather_top_rows(top0, 0)
         deal_top_rows(top0[:], planes[0], nc.sync)
 
-        hi_mask = held.tile([P, 1], I32, name="hi_mask")
-        nc.gpsimd.memset(hi_mask[:], HI_MASK)
-        upper = reused.tile([P, N, PACK], BF16, name="upper", offset=AT_TOP1, align_bytes=64)
+        upper = held.tile([P, N, PACK], BF16, name="upper", align_bytes=64)
         nc.scalar.copy(
             upper[:].rearrange("p (c i) j -> p c j i", i=4),
             raw[:].bitcast(BF16).rearrange("p j (c i two) -> p c j i two", i=4, two=2)[:, :, :, :, 1],
         )
         neg_hi_grouped = held.tile([P, N, PACK], BF16, name="neg_hi_grouped", align_bytes=64)
-        nc.vector.tensor_scalar(
-            out=neg_hi_grouped[:].rearrange("p n j -> p (n j)").bitcast(I32),
-            in0=upper[:].rearrange("p n j -> p (n j)").bitcast(I32),
-            scalar1=hi_mask[:],
-            scalar2=SIGN_BITS,
-            op0=ALU.bitwise_and,
-            op1=ALU.bitwise_xor,
-        )
-        neg_hi = held.tile([P, PACK, N], F32, name="neg_hi")
-        nc.scalar.activation(
-            out=neg_hi[:].rearrange("p j (c i) -> p c j i", i=4),
-            in_=neg_hi_grouped[:].rearrange("p (c i) j -> p c j i", i=4),
-            func=ACT.Copy,
-        )
+        neg_hi = []
+        for h in range(HALVES):
+            hi_mask = reused.tile([P, 1], I32, name=f"hi_mask{h}", offset=AT_TOP1 * (1 - h), align_bytes=64)
+            nc.gpsimd.memset(hi_mask[:], HI_MASK)
+            masked = neg_hi_grouped[:, h * M : (h + 1) * M]
+            nc.vector.tensor_scalar(
+                out=masked.rearrange("p n j -> p (n j)").bitcast(I32),
+                in0=upper[:, h * M : (h + 1) * M].rearrange("p n j -> p (n j)").bitcast(I32),
+                scalar1=hi_mask[:],
+                scalar2=SIGN_BITS,
+                op0=ALU.bitwise_and,
+                op1=ALU.bitwise_xor,
+            )
+        for h in range(HALVES):
+            neg_hi.append(held.tile([P, PACK, M], F32, name=f"neg_hi{h}"))
+            nc.scalar.activation(
+                out=neg_hi[h][:].rearrange("p j (c i) -> p c j i", i=4),
+                in_=neg_hi_grouped[:, h * M : (h + 1) * M].rearrange("p (c i) j -> p c j i", i=4),
+                func=ACT.Copy,
+            )
 
         word_win.append(held.tile([P, T], I32, name="word_win1", align_bytes=64))
         load_words(word_win[1], tab2_words, slice(0, 3 * T // 4))
@@ -123,12 +127,13 @@ def tile_list_cpxtab_hl_crelu_kernel(
 
         grouped[-1, 0] = neg_hi_grouped[:]
         turned = [psum.tile([M, PACK, P], F32, name=f"turned{h}", tag=f"bank2_{h}") for h in range(HALVES)]
-        for term, source in enumerate((raw, neg_hi)):
+        for term in range(2):
             for h in range(HALVES):
+                source = (raw[:, :, h * M : (h + 1) * M], neg_hi[h][:])[term]
                 for j in range(PACK):
                     nc.tensor.matmul(
                         turned[h][:, j],
-                        source[:, j, h * M : (h + 1) * M],
+                        source[:, j],
                         ident[:],
                         start=term == 0 and j == 0,
                         stop=term == 1 and j == PACK - 1,
@@ -212,12 +217,15 @@ def tile_list_cpxtab_hl_crelu_kernel(
             )
 
         def finish(acc, sign, out, half, s, on_vector):
-            res = stage.tile([M, W], F32, name="res")
-            if on_vector:
-                nc.vector.tensor_scalar(out=res[:], in0=acc[:], scalar1=sign, scalar2=0.0, op0=ALU.mult, op1=ALU.max)
-            else:
-                nc.scalar.activation(out=res[:], in_=acc[:], func=ACT.Relu, scale=sign)
-            nc.sync.dma_start(out[half * M : (half + 1) * M, s * W : (s + 1) * W], res[:])
+            step = W // 2 if s == SLICES - 1 and half == 0 and sign < 0 else W
+            for at in range(0, W, step):
+                res = stage.tile([M, step], F32, name="res")
+                part = acc[:, at : at + step]
+                if on_vector:
+                    nc.vector.tensor_scalar(out=res[:], in0=part, scalar1=sign, scalar2=0.0, op0=ALU.mult, op1=ALU.max)
+                else:
+                    nc.scalar.activation(out=res[:], in_=part, func=ACT.Relu, scale=sign)
+                nc.sync.dma_start(out[half * M : (half + 1) * M, s * W + at : s * W + at + step], res[:])
 
         re, im = {}, {}
 

@@ -25,10 +25,14 @@ W = 512
 SLICES = J // W
 ROWS = 16
 TOP = P - ROWS
+MID = 48
 HI_MASK = -((15 << 16) + 16)
 SIGN_BITS = -(1 << 31) + (1 << 15)
 AT_TOP1 = 2048
 AT_TOP0 = 7168
+AT_MASK = AT_TOP1 + 1024
+AT_NEG_HI = 16384
+AT_FIRST = 20480
 AT_TURNED = 8192
 AT_NEG_LO = 12288
 
@@ -40,7 +44,7 @@ def tile_list_cpxtab_hl_crelu_kernel(
     with ExitStack() as ctx:
         held = ctx.enter_context(tc.tile_pool(name="held", bufs=1))
         reused = ctx.enter_context(tc.tile_pool(name="reused", bufs=1))
-        stage = ctx.enter_context(tc.tile_pool(name="stage", bufs=17))
+        stage = ctx.enter_context(tc.tile_pool(name="stage", bufs=16))
         psum = ctx.enter_context(tc.psum_pool(name="psum", bufs=1))
 
         offsets = held.tile([P, J // 16], U16, name="offsets")
@@ -49,9 +53,11 @@ def tile_list_cpxtab_hl_crelu_kernel(
         wi_plane = held.tile([P, N // 4], I32, name="wi_plane", align_bytes=64)
         nc.vector.memset(wi_plane[:], 0)
         scale_win = [held.tile([P, T // 4], I32, name=f"scale_win{x}", align_bytes=64) for x in range(2)]
-        nc.vector.memset(scale_win[1][:], 0)
         nc.vector.memset(scale_win[0][:TOP], 0)
+        nc.vector.memset(scale_win[1][:MID], 0)
+        nc.gpsimd.memset(scale_win[1][MID + ROWS :], 0)
         nc.scalar.dma_start(scale_win[0][TOP:], tab_scales[0].bitcast(I32))
+        nc.sync.dma_start(scale_win[1][MID : MID + ROWS], tab2_scales[0].bitcast(I32))
         raw = held.tile([P, PACK, N], F32, name="raw")
         nc.sync.dma_start(raw[:], wr.rearrange("(p j) n -> p j n", j=PACK))
         planes = [
@@ -68,7 +74,6 @@ def tile_list_cpxtab_hl_crelu_kernel(
 
         word_win = [held.tile([P, T], I32, name="word_win0", align_bytes=64)]
         load_words(word_win[0], tab_words, slice(0, T))
-        nc.sync.dma_start(scale_win[1][4:P:8, :], tab2_scales[0].bitcast(I32))
 
         def picks(first, count):
             return offsets[:, first // 16 : (first + count) // 16]
@@ -89,16 +94,16 @@ def tile_list_cpxtab_hl_crelu_kernel(
             upper[:].rearrange("p (c i) j -> p c j i", i=4),
             raw[:].bitcast(BF16).rearrange("p j (c i two) -> p c j i two", i=4, two=2)[:, :, :, :, 1],
         )
-        neg_hi_grouped = held.tile([P, N, PACK], BF16, name="neg_hi_grouped", align_bytes=64)
+        neg_hi_grouped = reused.tile([P, N, PACK], BF16, name="neg_hi_grouped", offset=AT_NEG_HI, align_bytes=64)
         neg_hi = []
         for h in range(HALVES):
-            hi_mask = reused.tile([P, 1], I32, name=f"hi_mask{h}", offset=AT_TOP1 * (1 - h), align_bytes=64)
-            nc.gpsimd.memset(hi_mask[:], HI_MASK)
+            hi_mask = reused.tile([P, 32], I32, name=f"hi_mask{h}", offset=AT_MASK - 64 + 16384 * h, align_bytes=64)[:, :1]
+            nc.gpsimd.memset(hi_mask, HI_MASK)
             masked = neg_hi_grouped[:, h * M : (h + 1) * M]
             nc.vector.tensor_scalar(
                 out=masked.rearrange("p n j -> p (n j)").bitcast(I32),
                 in0=upper[:, h * M : (h + 1) * M].rearrange("p n j -> p (n j)").bitcast(I32),
-                scalar1=hi_mask[:],
+                scalar1=hi_mask,
                 scalar2=SIGN_BITS,
                 op0=ALU.bitwise_and,
                 op1=ALU.bitwise_xor,
@@ -141,7 +146,7 @@ def tile_list_cpxtab_hl_crelu_kernel(
                     )
         lo = []
         for h in range(HALVES):
-            lo_turned = reused.tile([M, PACK, P], F32, name=f"lo_turned{h}", offset=AT_TURNED + 2048 * h, align_bytes=64)
+            lo_turned = reused.tile([M, PACK, P], F32, name=f"lo_turned{h}", offset=(AT_FIRST + 1024, AT_TURNED)[h], align_bytes=64)
             nc.scalar.copy(lo_turned[:], turned[h][:])
             lo.append(psum.tile([P, PACK, M], F32, name=f"lo{h}", tag=f"bank3_{h}"))
             for j in range(PACK):
@@ -156,6 +161,8 @@ def tile_list_cpxtab_hl_crelu_kernel(
         top1 = reused.tile([P, J // 2], U8, name="top1", offset=AT_TOP1, align_bytes=64)
         gather_top_rows(top1, 1)
         deal_top_rows(top1[:, :W], planes[1], nc.sync)
+        first1 = reused.tile([P, W], U8, name="first1", offset=AT_MASK, align_bytes=64)
+        nc.vector.tensor_copy(first1[:], scale_win[1][:].bitcast(U8).indirect(picks(0, W)))
         for r in range(4):
             if r == 2:
                 load_words(word_win[1], tab2_words, slice(3 * T // 4, T))
@@ -217,15 +224,12 @@ def tile_list_cpxtab_hl_crelu_kernel(
             )
 
         def finish(acc, sign, out, half, s, on_vector):
-            step = W // 2 if s == SLICES - 1 and half == 0 and sign < 0 else W
-            for at in range(0, W, step):
-                res = stage.tile([M, step], F32, name="res")
-                part = acc[:, at : at + step]
-                if on_vector:
-                    nc.vector.tensor_scalar(out=res[:], in0=part, scalar1=sign, scalar2=0.0, op0=ALU.mult, op1=ALU.max)
-                else:
-                    nc.scalar.activation(out=res[:], in_=part, func=ACT.Relu, scale=sign)
-                nc.sync.dma_start(out[half * M : (half + 1) * M, s * W + at : s * W + at + step], res[:])
+            res = stage.tile([M, W], F32, name="res")
+            if on_vector:
+                nc.vector.tensor_scalar(out=res[:], in0=acc[:], scalar1=sign, scalar2=0.0, op0=ALU.mult, op1=ALU.max)
+            else:
+                nc.scalar.activation(out=res[:], in_=acc[:], func=ACT.Relu, scale=sign)
+            nc.sync.dma_start(out[half * M : (half + 1) * M, s * W : (s + 1) * W], res[:])
 
         re, im = {}, {}
 
@@ -255,20 +259,27 @@ def tile_list_cpxtab_hl_crelu_kernel(
                 finish(im[s, h], 1.0, out_1, h, s, s == SLICES - 1 and h == 1)
 
         quantise("neg_hi", grouped[-1, 0].rearrange("p n j -> p (n j)"), [(-1, 0)], None)
-        for s in range(2):
-            gather_words(0, s, f"slot{s}")
-            open_re(s, s)
+        wd[0, 0] = reused.tile([P, W], U32, name="wd0_0", offset=AT_FIRST, align_bytes=64)[:]
+        for h in range(HALVES):
+            re[0, h] = psum.tile([M, W], F32, name=f"re0_{h}", tag=f"bank0_{h}")
+        for first in (0, W // 2):
+            cols = slice(first, first + W // 2)
+            nc.vector.tensor_copy(wd[0, 0][:, cols], word_win[0][:].bitcast(U32).indirect(picks(first, W // 2)))
+            for h in range(HALVES):
+                rhs = wd[0, 0][:, cols].bitcast(FP8X4), sc[0, 0][:, cols]
+                mm(re[0, h][:, cols], wr_part(-1, 0, h), rhs, first == 0, False)
+        gather_words(0, 1, AT_FIRST + 2048)
+        open_re(1, 1)
         quantise("neg_lo", grouped[-1, 1].rearrange("p n j -> p (n j)"), [(-1, 1)], AT_TOP0)
         add_re(0)
         add_re(1)
-        gather_scales(0, AT_TOP0 + W)
         for r in range(4):
-            nc.sync.dma_start(planes[2][r:P:32, :], sc[1, 0][4 + 8 * r : P : 32].bitcast(I32))
+            nc.sync.dma_start(planes[2][r:P:32, :], first1[MID + r : MID + ROWS : 4].bitcast(I32))
         sc[1, 0] = planes[2].bitcast(U8)
         for r in range(4):
             nc.sync.dma_start(scale_win[1][r:P:32, :], tab2_scales[0, r:16:4, :].bitcast(I32))
         deal_top_rows(top1[:, W:], planes[3], nc.sync)
-        gather_words(0, 2, AT_NEG_LO + W)
+        gather_words(0, 2, AT_NEG_HI)
         open_re(2, 2)
         add_re(2)
         quantise("pos", pos_grouped[:].rearrange("p h n j -> p (h n j)"), [(1, 0), (1, 1)], AT_NEG_LO)

@@ -25,14 +25,14 @@ W = 512
 SLICES = J // W
 ROWS = 16
 TOP = P - ROWS
-MID = 48
-HI_MASK = -((15 << 16) + 16)
-SIGN_BITS = -(1 << 31) + (1 << 15)
+HI_MASK = -(1 << 20)
+SIGN_BIT = -(1 << 31)
 AT_TOP1 = 2048
 AT_TOP0 = 7168
 AT_MASK = AT_TOP1 + 1024
 AT_NEG_HI = 16384
 AT_FIRST = 20480
+AT_MASK1 = 24576
 AT_TURNED = 8192
 AT_NEG_LO = 12288
 
@@ -54,12 +54,11 @@ def tile_list_cpxtab_hl_crelu_kernel(
         nc.vector.memset(wi_plane[:], 0)
         scale_win = [held.tile([P, T // 4], I32, name=f"scale_win{x}", align_bytes=64) for x in range(2)]
         nc.vector.memset(scale_win[0][:TOP], 0)
-        nc.vector.memset(scale_win[1][:MID], 0)
-        nc.gpsimd.memset(scale_win[1][MID + ROWS :], 0)
-        nc.scalar.dma_start(scale_win[0][TOP:], tab_scales[0].bitcast(I32))
-        nc.sync.dma_start(scale_win[1][MID : MID + ROWS], tab2_scales[0].bitcast(I32))
+        nc.gpsimd.memset(scale_win[1][:TOP], 0)
+        nc.sync.dma_start(scale_win[0][TOP:], tab_scales[0].bitcast(I32))
         raw = held.tile([P, PACK, N], F32, name="raw")
         nc.sync.dma_start(raw[:], wr.rearrange("(p j) n -> p j n", j=PACK))
+        nc.sync.dma_start(scale_win[1][TOP:], tab2_scales[0].bitcast(I32))
         planes = [
             held.tile([P, width // 4], I32, name=f"plane{c}", align_bytes=64)[:] for c, width in enumerate((2 * W, W, W, W))
         ]
@@ -89,31 +88,17 @@ def tile_list_cpxtab_hl_crelu_kernel(
         gather_top_rows(top0, 0)
         deal_top_rows(top0[:], planes[0], nc.sync)
 
-        upper = held.tile([P, N, PACK], BF16, name="upper", align_bytes=64)
-        nc.scalar.copy(
-            upper[:].rearrange("p (c i) j -> p c j i", i=4),
-            raw[:].bitcast(BF16).rearrange("p j (c i two) -> p c j i two", i=4, two=2)[:, :, :, :, 1],
-        )
-        neg_hi_grouped = reused.tile([P, N, PACK], BF16, name="neg_hi_grouped", offset=AT_NEG_HI, align_bytes=64)
-        neg_hi = []
+        neg_hi = reused.tile([P, HALVES, PACK, M], F32, name="neg_hi", offset=AT_NEG_HI, align_bytes=64)
         for h in range(HALVES):
-            hi_mask = reused.tile([P, 32], I32, name=f"hi_mask{h}", offset=AT_MASK - 64 + 16384 * h, align_bytes=64)[:, :1]
+            hi_mask = reused.tile([P, 32], I32, name=f"hi_mask{h}", offset=(AT_MASK - 64, AT_MASK1)[h], align_bytes=64)[:, :1]
             nc.gpsimd.memset(hi_mask, HI_MASK)
-            masked = neg_hi_grouped[:, h * M : (h + 1) * M]
             nc.vector.tensor_scalar(
-                out=masked.rearrange("p n j -> p (n j)").bitcast(I32),
-                in0=upper[:, h * M : (h + 1) * M].rearrange("p n j -> p (n j)").bitcast(I32),
+                out=neg_hi[:, h].bitcast(I32),
+                in0=raw[:, :, h * M : (h + 1) * M].bitcast(I32),
                 scalar1=hi_mask,
-                scalar2=SIGN_BITS,
+                scalar2=SIGN_BIT,
                 op0=ALU.bitwise_and,
                 op1=ALU.bitwise_xor,
-            )
-        for h in range(HALVES):
-            neg_hi.append(held.tile([P, PACK, M], F32, name=f"neg_hi{h}"))
-            nc.scalar.activation(
-                out=neg_hi[h][:].rearrange("p j (c i) -> p c j i", i=4),
-                in_=neg_hi_grouped[:, h * M : (h + 1) * M].rearrange("p (c i) j -> p c j i", i=4),
-                func=ACT.Copy,
             )
 
         word_win.append(held.tile([P, T], I32, name="word_win1", align_bytes=64))
@@ -130,11 +115,21 @@ def tile_list_cpxtab_hl_crelu_kernel(
                     scale=float(sign),
                 )
 
-        grouped[-1, 0] = neg_hi_grouped[:]
+        def lay_hi(sign):
+            for h in range(HALVES):
+                nc.scalar.activation(
+                    out=grouped[sign, 0][:, h * M : (h + 1) * M].rearrange("p (c i) j -> p c j i", i=4),
+                    in_=neg_hi[:, h].rearrange("p j (c i) -> p c j i", i=4),
+                    func=ACT.Copy,
+                    scale=float(-sign),
+                )
+
+        grouped[-1, 0] = held.tile([P, N, PACK], BF16, name="neg_hi_grouped", align_bytes=64)[:]
+        lay_hi(-1)
         turned = [psum.tile([M, PACK, P], F32, name=f"turned{h}", tag=f"bank2_{h}") for h in range(HALVES)]
         for term in range(2):
             for h in range(HALVES):
-                source = (raw[:, :, h * M : (h + 1) * M], neg_hi[h][:])[term]
+                source = (raw[:, :, h * M : (h + 1) * M], neg_hi[:, h])[term]
                 for j in range(PACK):
                     nc.tensor.matmul(
                         turned[h][:, j],
@@ -155,7 +150,7 @@ def tile_list_cpxtab_hl_crelu_kernel(
         lay_lo(-1)
         pos_grouped = reused.tile([P, 2, N, PACK], BF16, name="pos_grouped", offset=AT_TURNED, align_bytes=64)
         grouped[1, 0], grouped[1, 1] = pos_grouped[:, 0], pos_grouped[:, 1]
-        nc.scalar.activation(out=grouped[1, 0], in_=grouped[-1, 0], func=ACT.Copy, scale=-1.0)
+        lay_hi(1)
         lay_lo(1)
 
         top1 = reused.tile([P, J // 2], U8, name="top1", offset=AT_TOP1, align_bytes=64)
@@ -273,8 +268,7 @@ def tile_list_cpxtab_hl_crelu_kernel(
         quantise("neg_lo", grouped[-1, 1].rearrange("p n j -> p (n j)"), [(-1, 1)], AT_TOP0)
         add_re(0)
         add_re(1)
-        for r in range(4):
-            nc.sync.dma_start(planes[2][r:P:32, :], first1[MID + r : MID + ROWS : 4].bitcast(I32))
+        deal_top_rows(first1[:], planes[2], nc.sync)
         sc[1, 0] = planes[2].bitcast(U8)
         for r in range(4):
             nc.sync.dma_start(scale_win[1][r:P:32, :], tab2_scales[0, r:16:4, :].bitcast(I32))

@@ -24,7 +24,7 @@ HALVES = N // M
 W = 512
 SLICES = J // W
 ROWS = 16
-TOP = P - ROWS
+SPREAD = slice(32, 96, 4)
 HI_MASK = -(1 << 20)
 SIGN_BIT = -(1 << 31)
 AT_TOP1 = 2048
@@ -50,17 +50,19 @@ def tile_list_cpxtab_hl_crelu_kernel(
         offsets = held.tile([P, J // 16], U16, name="offsets")
         nc.sync.dma_start(offsets[:], offs)
 
+        raw = held.tile([P, PACK, N], F32, name="raw")
+        wr_rows = wr.rearrange("(p j) n -> p j n", j=PACK)
+        nc.sync.dma_start(raw[:, :2], wr_rows[:, :2])
+        scale_win = [held.tile([P, T // 4], I32, name=f"scale_win{x}", align_bytes=64) for x in range(2)]
+        nc.vector.memset(scale_win[0][:], 0)
+        nc.sync.dma_start(scale_win[0][SPREAD], tab_scales[0].bitcast(I32))
+        nc.sync.dma_start(raw[:, 2:], wr_rows[:, 2:])
+        nc.vector.memset(scale_win[1][:], 0)
+        nc.sync.dma_start(scale_win[1][SPREAD], tab2_scales[0].bitcast(I32))
         wi_plane = held.tile([P, N // 4], I32, name="wi_plane", align_bytes=64)
         nc.vector.memset(wi_plane[:], 0)
-        scale_win = [held.tile([P, T // 4], I32, name=f"scale_win{x}", align_bytes=64) for x in range(2)]
-        nc.vector.memset(scale_win[0][:TOP], 0)
-        nc.gpsimd.memset(scale_win[1][:TOP], 0)
-        nc.sync.dma_start(scale_win[0][TOP:], tab_scales[0].bitcast(I32))
-        raw = held.tile([P, PACK, N], F32, name="raw")
-        nc.sync.dma_start(raw[:], wr.rearrange("(p j) n -> p j n", j=PACK))
-        nc.sync.dma_start(scale_win[1][TOP:], tab2_scales[0].bitcast(I32))
         planes = [
-            held.tile([P, width // 4], I32, name=f"plane{c}", align_bytes=64)[:] for c, width in enumerate((2 * W, W, W, W))
+            held.tile([P, width // 4], I32, name=f"plane{c}", align_bytes=64)[:] for c, width in enumerate((2 * W, 2 * W, W))
         ]
         for plane in planes:
             nc.vector.memset(plane, 0)
@@ -78,14 +80,14 @@ def tile_list_cpxtab_hl_crelu_kernel(
             return offsets[:, first // 16 : (first + count) // 16]
 
         def gather_top_rows(got, half):
-            nc.vector.tensor_copy(got[:], scale_win[0][:].bitcast(U8).indirect(picks(half * J // 2, J // 2)))
+            nc.vector.tensor_copy(got, scale_win[0][:].bitcast(U8).indirect(picks(half * J // 2, J // 2)))
 
         def deal_top_rows(got, plane, queue):
             for r in range(4):
-                queue.dma_start(plane[r:P:32, :], got[TOP + r : P : 4].bitcast(I32))
+                queue.dma_start(plane[r:P:32, :], got[32 + 4 * r : 96 : 16].bitcast(I32))
 
         top0 = reused.tile([P, J // 2], U8, name="top0", offset=AT_TOP0, align_bytes=64)
-        gather_top_rows(top0, 0)
+        gather_top_rows(top0[:], 0)
         deal_top_rows(top0[:], planes[0], nc.sync)
 
         neg_hi = reused.tile([P, HALVES, PACK, M], F32, name="neg_hi", offset=AT_NEG_HI, align_bytes=64)
@@ -153,11 +155,10 @@ def tile_list_cpxtab_hl_crelu_kernel(
         lay_hi(1)
         lay_lo(1)
 
-        top1 = reused.tile([P, J // 2], U8, name="top1", offset=AT_TOP1, align_bytes=64)
-        gather_top_rows(top1, 1)
-        deal_top_rows(top1[:, :W], planes[1], nc.sync)
-        first1 = reused.tile([P, W], U8, name="first1", offset=AT_MASK, align_bytes=64)
-        nc.vector.tensor_copy(first1[:], scale_win[1][:].bitcast(U8).indirect(picks(0, W)))
+        top1 = reused.tile([P, 3 * W], U8, name="top1", offset=AT_TOP1, align_bytes=64)
+        gather_top_rows(top1[:, W:], 1)
+        nc.vector.tensor_copy(top1[:, :W], scale_win[1][:].bitcast(U8).indirect(picks(0, W)))
+        deal_top_rows(top1[:, : 2 * W], planes[1], nc.sync)
         for r in range(4):
             if r == 2:
                 load_words(word_win[1], tab2_words, slice(3 * T // 4, T))
@@ -190,7 +191,7 @@ def tile_list_cpxtab_hl_crelu_kernel(
         sc, wd = {}, {}
         for s in range(2):
             sc[0, s] = planes[0][:, s * W // 4 : (s + 1) * W // 4].bitcast(U8)
-        sc[0, 2], sc[0, 3] = planes[1].bitcast(U8), planes[3].bitcast(U8)
+        sc[1, 0], sc[0, 2], sc[0, 3] = planes[1][:, : W // 4].bitcast(U8), planes[1][:, W // 4 :].bitcast(U8), planes[2].bitcast(U8)
 
         def gather_scales(s, slot):
             if isinstance(slot, int):
@@ -268,11 +269,9 @@ def tile_list_cpxtab_hl_crelu_kernel(
         quantise("neg_lo", grouped[-1, 1].rearrange("p n j -> p (n j)"), [(-1, 1)], AT_TOP0)
         add_re(0)
         add_re(1)
-        deal_top_rows(first1[:], planes[2], nc.sync)
-        sc[1, 0] = planes[2].bitcast(U8)
         for r in range(4):
             nc.sync.dma_start(scale_win[1][r:P:32, :], tab2_scales[0, r:16:4, :].bitcast(I32))
-        deal_top_rows(top1[:, W:], planes[3], nc.sync)
+        deal_top_rows(top1[:, 2 * W :], planes[2], nc.sync)
         gather_words(0, 2, AT_NEG_HI)
         open_re(2, 2)
         add_re(2)

@@ -24,6 +24,7 @@ HALVES = N // M
 W = 512
 SLICES = J // W
 ROWS = 16
+TOP = P - ROWS
 SPREAD = slice(32, 96, 4)
 HI_MASK = -(1 << 20)
 SIGN_BIT = -(1 << 31)
@@ -50,19 +51,17 @@ def tile_list_cpxtab_hl_crelu_kernel(
         offsets = held.tile([P, J // 16], U16, name="offsets")
         nc.sync.dma_start(offsets[:], offs)
 
-        raw = held.tile([P, PACK, N], F32, name="raw")
-        wr_rows = wr.rearrange("(p j) n -> p j n", j=PACK)
-        nc.sync.dma_start(raw[:, :2], wr_rows[:, :2])
         scale_win = [held.tile([P, T // 4], I32, name=f"scale_win{x}", align_bytes=64) for x in range(2)]
-        nc.vector.memset(scale_win[0][:], 0)
-        nc.sync.dma_start(scale_win[0][SPREAD], tab_scales[0].bitcast(I32))
-        nc.sync.dma_start(raw[:, 2:], wr_rows[:, 2:])
         nc.vector.memset(scale_win[1][:], 0)
-        nc.sync.dma_start(scale_win[1][SPREAD], tab2_scales[0].bitcast(I32))
+        nc.vector.memset(scale_win[0][:TOP], 0)
         wi_plane = held.tile([P, N // 4], I32, name="wi_plane", align_bytes=64)
         nc.vector.memset(wi_plane[:], 0)
+        nc.sync.dma_start(scale_win[0][TOP:], tab_scales[0].bitcast(I32))
+        raw = held.tile([P, PACK, N], F32, name="raw")
+        nc.sync.dma_start(raw[:], wr.rearrange("(p j) n -> p j n", j=PACK))
+        nc.sync.dma_start(scale_win[1][SPREAD], tab2_scales[0].bitcast(I32))
         planes = [
-            held.tile([P, width // 4], I32, name=f"plane{c}", align_bytes=64)[:] for c, width in enumerate((2 * W, 2 * W, W))
+            held.tile([P, width // 4], I32, name=f"plane{c}", align_bytes=64)[:] for c, width in enumerate((2 * W, W, W, W))
         ]
         for plane in planes:
             nc.vector.memset(plane, 0)
@@ -80,14 +79,14 @@ def tile_list_cpxtab_hl_crelu_kernel(
             return offsets[:, first // 16 : (first + count) // 16]
 
         def gather_top_rows(got, half):
-            nc.vector.tensor_copy(got, scale_win[0][:].bitcast(U8).indirect(picks(half * J // 2, J // 2)))
+            nc.vector.tensor_copy(got[:], scale_win[0][:].bitcast(U8).indirect(picks(half * J // 2, J // 2)))
 
         def deal_top_rows(got, plane, queue):
             for r in range(4):
-                queue.dma_start(plane[r:P:32, :], got[32 + 4 * r : 96 : 16].bitcast(I32))
+                queue.dma_start(plane[r:P:32, :], got[TOP + r : P : 4].bitcast(I32))
 
         top0 = reused.tile([P, J // 2], U8, name="top0", offset=AT_TOP0, align_bytes=64)
-        gather_top_rows(top0[:], 0)
+        gather_top_rows(top0, 0)
         deal_top_rows(top0[:], planes[0], nc.sync)
 
         neg_hi = reused.tile([P, HALVES, PACK, M], F32, name="neg_hi", offset=AT_NEG_HI, align_bytes=64)
@@ -155,10 +154,11 @@ def tile_list_cpxtab_hl_crelu_kernel(
         lay_hi(1)
         lay_lo(1)
 
-        top1 = reused.tile([P, 3 * W], U8, name="top1", offset=AT_TOP1, align_bytes=64)
-        gather_top_rows(top1[:, W:], 1)
-        nc.vector.tensor_copy(top1[:, :W], scale_win[1][:].bitcast(U8).indirect(picks(0, W)))
-        deal_top_rows(top1[:, : 2 * W], planes[1], nc.sync)
+        top1 = reused.tile([P, J // 2], U8, name="top1", offset=AT_TOP1, align_bytes=64)
+        gather_top_rows(top1, 1)
+        deal_top_rows(top1[:, :W], planes[1], nc.sync)
+        first1 = reused.tile([P, W], U8, name="first1", offset=AT_MASK, align_bytes=64)
+        nc.vector.tensor_copy(first1[:], scale_win[1][:].bitcast(U8).indirect(picks(0, W)))
         for r in range(4):
             if r == 2:
                 load_words(word_win[1], tab2_words, slice(3 * T // 4, T))
@@ -191,7 +191,7 @@ def tile_list_cpxtab_hl_crelu_kernel(
         sc, wd = {}, {}
         for s in range(2):
             sc[0, s] = planes[0][:, s * W // 4 : (s + 1) * W // 4].bitcast(U8)
-        sc[1, 0], sc[0, 2], sc[0, 3] = planes[1][:, : W // 4].bitcast(U8), planes[1][:, W // 4 :].bitcast(U8), planes[2].bitcast(U8)
+        sc[0, 2], sc[0, 3] = planes[1].bitcast(U8), planes[3].bitcast(U8)
 
         def gather_scales(s, slot):
             if isinstance(slot, int):
@@ -270,8 +270,11 @@ def tile_list_cpxtab_hl_crelu_kernel(
         add_re(0)
         add_re(1)
         for r in range(4):
+            nc.sync.dma_start(planes[2][r:P:32, :], first1[32 + 4 * r : 96 : 16].bitcast(I32))
+        sc[1, 0] = planes[2].bitcast(U8)
+        for r in range(4):
             nc.sync.dma_start(scale_win[1][r:P:32, :], tab2_scales[0, r:16:4, :].bitcast(I32))
-        deal_top_rows(top1[:, 2 * W :], planes[2], nc.sync)
+        deal_top_rows(top1[:, W:], planes[3], nc.sync)
         gather_words(0, 2, AT_NEG_HI)
         open_re(2, 2)
         add_re(2)

@@ -29,7 +29,7 @@ SPREAD = slice(32, 96, 4)
 HI_MASK = -(1 << 20)
 SIGN_BIT = -(1 << 31)
 AT_TOP1 = 2048
-AT_TOP0 = 7168
+AT_TOP0 = 28672
 AT_MASK = AT_TOP1 + 1024
 AT_NEG_HI = 16384
 AT_FIRST = 20480
@@ -264,10 +264,10 @@ def tile_list_cpxtab_hl_crelu_kernel(
             for h in range(HALVES):
                 rhs = wd[0, 0][:, cols].bitcast(FP8X4), sc[0, 0][:, cols]
                 mm(re[0, h][:, cols], wr_part(-1, 0, h), rhs, first == 0, False)
-        gather_words(0, 1, AT_FIRST + 2048)
-        open_re(1, 1)
         quantise("neg_lo", grouped[-1, 1].rearrange("p n j -> p (n j)"), [(-1, 1)], AT_TOP0)
         add_re(0)
+        gather_words(0, 1, AT_TOP0 + 512)
+        open_re(1, 1)
         add_re(1)
         for r in range(4):
             nc.sync.dma_start(planes[2][r:P:32, :], first1[32 + 4 * r : 96 : 16].bitcast(I32))

from contextlib import ExitStack

import concourse.mybir as mybir
from concourse.masks import make_identity

K, N, T, J = 512, 256, 4096, 2048
FLOPS = 6 * 2 * K * N * J

F32 = mybir.dt.float32
BF16 = mybir.dt.bfloat16
I32 = mybir.dt.int32
U32 = mybir.dt.uint32
U16 = mybir.dt.uint16
U8 = mybir.dt.uint8
FP8X4 = mybir.dt.float8_e4m3fn_x4
FP4X4 = mybir.dt.float4_e2m1fn_x4
ALU = mybir.AluOpType
ACT = mybir.ActivationFunctionType

P = 128
PACK = 4
M = 128
HALVES = N // M
W = 512
SLICES = J // W
ROWS = 16
TOP = P - ROWS
SPREAD = slice(32, 96, 4)
HI_MASK = -(1 << 20)
SIGN_BIT = -(1 << 31)
AT_TOP1 = 2048
AT_TOP0 = 28672
AT_MASK = AT_TOP1 + 1024
AT_NEG_HI = 16384
AT_FIRST = 20480
AT_MASK1 = 24576
AT_TURNED = 8192
AT_NEG_LO = 12288


def tile_list_cpxtab_hl_crelu_kernel(
    tc, tab_words, tab_scales, tab2_words, tab2_scales, wr, wi_words, wi_scales, offs, out_0, out_1
):
    nc = tc.nc
    with ExitStack() as ctx:
        held = ctx.enter_context(tc.tile_pool(name="held", bufs=1))
        reused = ctx.enter_context(tc.tile_pool(name="reused", bufs=1))
        stage = ctx.enter_context(tc.tile_pool(name="stage", bufs=16))
        psum = ctx.enter_context(tc.psum_pool(name="psum", bufs=1))

        offsets = held.tile([P, J // 16], U16, name="offsets")
        nc.sync.dma_start(offsets[:], offs)

        scale_win = [held.tile([P, T // 4], I32, name=f"scale_win{x}", align_bytes=64) for x in range(2)]
        nc.vector.memset(scale_win[1][:], 0)
        nc.vector.memset(scale_win[0][:TOP], 0)
        wi_plane = held.tile([P, N // 4], I32, name="wi_plane", align_bytes=64)
        nc.vector.memset(wi_plane[:], 0)
        nc.sync.dma_start(scale_win[0][TOP:], tab_scales[0].bitcast(I32))
        raw = held.tile([P, PACK, N], F32, name="raw")
        nc.sync.dma_start(raw[:], wr.rearrange("(p j) n -> p j n", j=PACK))
        nc.sync.dma_start(scale_win[1][SPREAD], tab2_scales[0].bitcast(I32))
        planes = [
            held.tile([P, width // 4], I32, name=f"plane{c}", align_bytes=64)[:] for c, width in enumerate((2 * W, W, W, W))
        ]
        for plane in planes:
            nc.vector.memset(plane, 0)

        ident = held.tile([P, P], F32, name="ident")
        make_identity(nc, ident[:])

        def load_words(win, words, cols):
            nc.sync.dma_start(win[:, cols], words[0].rearrange("p t i -> p (t i)").bitcast(I32)[:, cols])

        word_win = [held.tile([P, T], I32, name="word_win0", align_bytes=64)]
        load_words(word_win[0], tab_words, slice(0, T))

        def picks(first, count):
            return offsets[:, first // 16 : (first + count) // 16]

        def gather_top_rows(got, half):
            nc.vector.tensor_copy(got[:], scale_win[0][:].bitcast(U8).indirect(picks(half * J // 2, J // 2)))

        def deal_top_rows(got, plane, queue):
            for r in range(4):
                queue.dma_start(plane[r:P:32, :], got[TOP + r : P : 4].bitcast(I32))

        top0 = reused.tile([P, J // 2], U8, name="top0", offset=AT_TOP0, align_bytes=64)
        gather_top_rows(top0, 0)
        deal_top_rows(top0[:], planes[0], nc.sync)

        neg_hi = reused.tile([P, HALVES, PACK, M], F32, name="neg_hi", offset=AT_NEG_HI, align_bytes=64)
        for h in range(HALVES):
            hi_mask = reused.tile([P, 32], I32, name=f"hi_mask{h}", offset=(AT_MASK - 64, AT_MASK1)[h], align_bytes=64)[:, :1]
            nc.gpsimd.memset(hi_mask, HI_MASK)
            nc.vector.tensor_scalar(
                out=neg_hi[:, h].bitcast(I32),
                in0=raw[:, :, h * M : (h + 1) * M].bitcast(I32),
                scalar1=hi_mask,
                scalar2=SIGN_BIT,
                op0=ALU.bitwise_and,
                op1=ALU.bitwise_xor,
            )

        word_win.append(held.tile([P, T], I32, name="word_win1", align_bytes=64))
        load_words(word_win[1], tab2_words, slice(0, 3 * T // 4))

        grouped, codes, code_scales = {}, {}, {}

        def lay_lo(sign):
            for h in range(HALVES):
                nc.scalar.activation(
                    out=grouped[sign, 1][:, h * M : (h + 1) * M],
                    in_=lo[h][:].rearrange("p j n -> p n j"),
                    func=ACT.Copy,
                    scale=float(sign),
                )

        def lay_hi(sign):
            for h in range(HALVES):
                nc.scalar.activation(
                    out=grouped[sign, 0][:, h * M : (h + 1) * M].rearrange("p (c i) j -> p c j i", i=4),
                    in_=neg_hi[:, h].rearrange("p j (c i) -> p c j i", i=4),
                    func=ACT.Copy,
                    scale=float(-sign),
                )

        grouped[-1, 0] = held.tile([P, N, PACK], BF16, name="neg_hi_grouped", align_bytes=64)[:]
        lay_hi(-1)
        turned = [psum.tile([M, PACK, P], F32, name=f"turned{h}", tag=f"bank2_{h}") for h in range(HALVES)]
        for term in range(2):
            for h in range(HALVES):
                source = (raw[:, :, h * M : (h + 1) * M], neg_hi[:, h])[term]
                for j in range(PACK):
                    nc.tensor.matmul(
                        turned[h][:, j],
                        source[:, j],
                        ident[:],
                        start=term == 0 and j == 0,
                        stop=term == 1 and j == PACK - 1,
                        is_transpose=True,
                    )
        lo = []
        for h in range(HALVES):
            lo_turned = reused.tile([M, PACK, P], F32, name=f"lo_turned{h}", offset=(AT_FIRST + 1024, AT_TURNED)[h], align_bytes=64)
            nc.scalar.copy(lo_turned[:], turned[h][:])
            lo.append(psum.tile([P, PACK, M], F32, name=f"lo{h}", tag=f"bank3_{h}"))
            for j in range(PACK):
                nc.tensor.transpose(lo[h][:, j], lo_turned[:, j], ident[:])
        grouped[-1, 1] = reused.tile([P, N, PACK], BF16, name="neg_lo_grouped", offset=AT_NEG_LO, align_bytes=64)[:]
        lay_lo(-1)
        pos_grouped = reused.tile([P, 2, N, PACK], BF16, name="pos_grouped", offset=AT_TURNED, align_bytes=64)
        grouped[1, 0], grouped[1, 1] = pos_grouped[:, 0], pos_grouped[:, 1]
        lay_hi(1)
        lay_lo(1)

        top1 = reused.tile([P, J // 2], U8, name="top1", offset=AT_TOP1, align_bytes=64)
        gather_top_rows(top1, 1)
        deal_top_rows(top1[:, :W], planes[1], nc.sync)
        first1 = reused.tile([P, W], U8, name="first1", offset=AT_MASK, align_bytes=64)
        nc.vector.tensor_copy(first1[:], scale_win[1][:].bitcast(U8).indirect(picks(0, W)))
        for r in range(4):
            if r == 2:
                load_words(word_win[1], tab2_words, slice(3 * T // 4, T))
            nc.sync.dma_start(wi_plane[r:P:32, :], wi_scales[0, r:16:4, :].bitcast(I32))
        wi_codes = held.tile([P, N // 2], I32, name="wi_codes", align_bytes=64)
        nc.sync.dma_start(wi_codes[:], wi_words[0].bitcast(I32))

        def quantise(name, values, keys, at):
            width = N * len(keys)
            words = held.tile([P, width], U32, name=f"{name}_codes", align_bytes=64)
            if at is None:
                scales = held.tile([P, width], U8, name=f"{name}_scales", align_bytes=64)
            else:
                scales = reused.tile([P, width], U8, name=f"{name}_scales", offset=at, align_bytes=64)
            nc.vector.quantize_mx(out=words[:].bitcast(FP8X4), scales=scales[:], in_=values)
            for place, key in enumerate(keys):
                codes[key] = words[:, place * N : (place + 1) * N]
                code_scales[key] = scales[:, place * N : (place + 1) * N]

        def wr_part(sign, part, half):
            cols = slice(half * M, (half + 1) * M)
            return codes[sign, part][:, cols].bitcast(FP8X4), code_scales[sign, part][:, cols]

        def wi_part(half):
            return (
                wi_codes[:, half * 64 : (half + 1) * 64].bitcast(FP4X4),
                wi_plane[:, half * 32 : (half + 1) * 32].bitcast(U8),
            )

        sc, wd = {}, {}
        for s in range(2):
            sc[0, s] = planes[0][:, s * W // 4 : (s + 1) * W // 4].bitcast(U8)
        sc[0, 2], sc[0, 3] = planes[1].bitcast(U8), planes[3].bitcast(U8)

        def gather_scales(s, slot):
            if isinstance(slot, int):
                got = reused.tile([P, W], U8, name=f"sc1_{s}", offset=slot, align_bytes=64)
            else:
                got = held.tile([P, W], U8, name=f"sc1_{s}", tag=slot, align_bytes=64)
            nc.vector.tensor_copy(got[:], scale_win[1][:].bitcast(U8).indirect(picks(s * W, W)))
            sc[1, s] = got[:]

        def gather_words(x, s, slot):
            if isinstance(slot, int):
                got = reused.tile([P, W], U32, name=f"wd{x}_{s}", offset=slot, align_bytes=64)[:]
            elif isinstance(slot, str):
                got = held.tile([P, W], U32, name=f"wd{x}_{s}", tag=slot, align_bytes=64)[:]
            else:
                got = slot
            nc.vector.tensor_copy(got, word_win[x][:].bitcast(U32).indirect(picks(s * W, W)))
            wd[x, s] = got

        def operand(x, s):
            return wd[x, s].bitcast(FP8X4), sc[x, s]

        def mm(acc, lhs, rhs, start, stop):
            nc.tensor.matmul_mx(
                out=acc[:], lhsT=lhs[0], lhsT_scale=lhs[1], rhs=rhs[0], rhs_scale=rhs[1], start=start, stop=stop
            )

        def finish(acc, sign, out, half, s, on_vector):
            res = stage.tile([M, W], F32, name="res")
            if on_vector:
                nc.vector.tensor_scalar(out=res[:], in0=acc[:], scalar1=sign, scalar2=0.0, op0=ALU.mult, op1=ALU.max)
            else:
                nc.scalar.activation(out=res[:], in_=acc[:], func=ACT.Relu, scale=sign)
            nc.sync.dma_start(out[half * M : (half + 1) * M, s * W : (s + 1) * W], res[:])

        re, im = {}, {}

        def open_re(s, pair):
            for h in range(HALVES):
                re[s, h] = psum.tile([M, W], F32, name=f"re{s}_{h}", tag=f"bank{pair}_{h}")
                mm(re[s, h], wr_part(-1, 0, h), operand(0, s), True, False)

        def add_re(s):
            for h in range(HALVES):
                mm(re[s, h], wr_part(-1, 1, h), operand(0, s), False, False)

        def open_im(s, pair):
            for h in range(HALVES):
                im[s, h] = psum.tile([M, W], F32, name=f"im{s}_{h}", tag=f"bank{pair}_{h}")
                mm(im[s, h], wi_part(h), operand(0, s), True, False)

        def close_re(s):
            for h in range(HALVES):
                mm(re[s, h], wi_part(h), operand(1, s), False, True)
                finish(re[s, h], -1.0, out_0, h, s, s == SLICES - 1 and h == 1)

        def close_im(s):
            for h in range(HALVES):
                mm(im[s, h], wr_part(1, 0, h), operand(1, s), False, False)
                mm(im[s, h], wr_part(1, 1, h), operand(1, s), False, True)
                finish(im[s, h], 1.0, out_1, h, s, s == SLICES - 1 and h == 1)

        quantise("neg_hi", grouped[-1, 0].rearrange("p n j -> p (n j)"), [(-1, 0)], None)
        wd[0, 0] = reused.tile([P, W], U32, name="wd0_0", offset=AT_FIRST, align_bytes=64)[:]
        for h in range(HALVES):
            re[0, h] = psum.tile([M, W], F32, name=f"re0_{h}", tag=f"bank0_{h}")
        for first in (0, W // 2):
            cols = slice(first, first + W // 2)
            nc.vector.tensor_copy(wd[0, 0][:, cols], word_win[0][:].bitcast(U32).indirect(picks(first, W // 2)))
            for h in range(HALVES):
                rhs = wd[0, 0][:, cols].bitcast(FP8X4), sc[0, 0][:, cols]
                mm(re[0, h][:, cols], wr_part(-1, 0, h), rhs, first == 0, False)
        quantise("neg_lo", grouped[-1, 1].rearrange("p n j -> p (n j)"), [(-1, 1)], AT_TOP0)
        add_re(0)
        gather_words(0, 1, AT_TOP0 + 512)
        open_re(1, 1)
        add_re(1)
        for r in range(4):
            nc.sync.dma_start(planes[2][r:P:32, :], first1[32 + 4 * r : 96 : 16].bitcast(I32))
        sc[1, 0] = planes[2].bitcast(U8)
        for r in range(4):
            nc.sync.dma_start(scale_win[1][r:P:32, :], tab2_scales[0, r:16:4, :].bitcast(I32))
        deal_top_rows(top1[:, W:], planes[3], nc.sync)
        gather_words(0, 2, AT_NEG_HI)
        open_re(2, 2)
        add_re(2)
        quantise("pos", pos_grouped[:].rearrange("p h n j -> p (h n j)"), [(1, 0), (1, 1)], AT_NEG_LO)
        open_im(0, 3)
        gather_words(1, 0, "slot4")
        close_re(0)
        close_im(0)
        open_im(1, 0)
        gather_words(1, 1, "slot5")
        gather_scales(1, "second1")
        close_re(1)
        close_im(1)
        open_im(2, 3)
        gather_words(1, 2, AT_TOP1 + 256 - 4 * W)
        gather_scales(2, "second2")
        close_re(2)
        close_im(2)
        last = reused.tile([P, 2 * W], U32, name="last_words", offset=AT_TOP1 + 256 + W, align_bytes=64)
        gather_words(0, 3, last[:, :W])
        open_re(3, 1)
        add_re(3)
        open_im(3, 0)
        gather_scales(3, AT_TOP1 + 256)
        gather_words(1, 3, last[:, W:])
        close_re(3)
        close_im(3)
